import numpy as np
import ml_dtypes


def mxq(x, axis, fmt="e4m3"):
    dtype, down = {"e4m3": (ml_dtypes.float8_e4m3fn, 7), "e5m2": (ml_dtypes.float8_e5m2, 14)}[fmt]
    v = np.moveaxis(np.asarray(x, np.float32).astype(ml_dtypes.bfloat16).astype(np.float64), axis, -1)
    blocks = v.reshape(v.shape[:-1] + (-1, 32))
    amax = np.abs(blocks).max(-1, keepdims=True)
    byte = np.maximum(np.where(amax > 0, np.frexp(amax)[1] - 1 + 127, 0) - down, 1)
    scale = np.exp2(byte - 127.0)
    codes = (blocks / scale).astype(np.float32).astype(dtype).astype(np.float64)
    return np.moveaxis((codes * scale).reshape(v.shape), -1, axis)


WIDE = False


def mx_kscale(k):
    if not WIDE:
        return np.ones(k)
    levels = np.array([24, -24, 12, -12, 0])
    if k % 512:
        return np.exp2(np.random.permutation(np.resize(levels, k // 32))).repeat(32)
    a = np.empty((k // 512, 16))
    for p in range(k // 512):
        a[p, :8] = np.random.permutation(np.resize(levels, 8))
        for g in range(8):
            far = levels[np.abs(levels - a[p, g]) >= 10]
            a[p, g + 8] = far[np.random.randint(len(far))]
    return np.exp2(a.ravel()).repeat(32)


def f64(x):
    return np.asarray(x).astype(np.float64)


def striped(idx):
    return np.tile(idx.reshape(-1, 16).T, (8, 1)).astype(np.uint16)


def unstriped(offs):
    return offs[:16].T.reshape(-1).astype(np.int64)


E2M1 = np.array([0.0, 0.5, 1.0, 1.5, 2.0, 3.0, 4.0, 6.0, -0.0, -0.5, -1.0, -1.5, -2.0, -3.0, -4.0, -6.0])


def pack_weight(w, fmt):
    k, n = w.shape
    w = f64(np.asarray(w, np.float32).astype(ml_dtypes.bfloat16)).reshape(k // 32, 32, n)
    amax = np.abs(w).max(1)
    if fmt == "e4m3":
        byte = np.frexp(amax)[1] - 1 + 127 - 7
    else:
        mant, ex = np.frexp(amax / 6.0)
        byte = np.where(mant > 0.5, ex, ex - 1) + 127
    byte = np.clip(np.where(amax > 0, byte, 1), 1, 254)
    scaled = (w * np.exp2(127.0 - byte)[:, None, :]).reshape(k, n).astype(np.float32)
    by_word = np.ascontiguousarray(scaled.reshape(k // 512, 128, 4, n).transpose(0, 1, 3, 2))
    if fmt == "e4m3":
        words = by_word.astype(ml_dtypes.float8_e4m3fn).view(np.uint8)
    else:
        c = by_word.astype(ml_dtypes.float4_e2m1fn).view(np.uint8) & 0xF
        words = (c[..., 0::2] | (c[..., 1::2] << 4)).reshape(k // 512, 128, 2 * n)
    return np.ascontiguousarray(words), np.ascontiguousarray(byte.astype(np.uint8).reshape(k // 512, 16, n))


def unpack_weight(words, scales, fmt):
    g, _, n = scales.shape
    words = np.ascontiguousarray(words).reshape(g, 128, n, -1)
    if fmt == "e4m3":
        vals = words.view(ml_dtypes.float8_e4m3fn).astype(np.float64)
    else:
        nib = np.empty((g, 128, n, 4), np.uint8)
        nib[..., 0::2] = words & 0xF
        nib[..., 1::2] = words >> 4
        vals = E2M1[nib]
    vals = vals * np.repeat(np.exp2(scales.astype(np.float64) - 127.0), 8, axis=1)[..., None]
    return vals.transpose(0, 1, 3, 2).reshape(g * 512, n)


def silu(f):
    return f / (1.0 + np.exp(-np.maximum(f, -700.0)))


K, R, N, T, J = 512, 512, 512, 2048, 1024


def setup_inputs():
    n = np.random.standard_normal
    s = mx_kscale(K)[:, None]
    u = mx_kscale(R)[:, None]
    p_tab = pack_weight(n((K, T)) * s, "e4m3")
    p_ws = pack_weight(n((K, R)) / np.sqrt(2 * K) / s, "e4m3")
    p_wt = pack_weight(n((K, R)) / np.sqrt(2 * K) / s, "e4m3")
    return {
        "tab_words": p_tab[0],
        "tab_scales": p_tab[1],
        "ws_words": p_ws[0],
        "ws_scales": p_ws[1],
        "wt_words": p_wt[0],
        "wt_scales": p_wt[1],
        "sm": (np.random.uniform(0.5, 2.0, R) * u[:, 0]).astype(np.float32),
        "wd": (n((R, N)) / np.sqrt(R) / u).astype(np.float32),
        "wgo": np.tile(np.random.uniform(0.5, 2.0, J), (128, 1)).astype(np.float32),
        "offs": striped(np.random.permutation(T)[:J]),
        "offs2": striped(np.random.permutation(T)[:J]),
    }


def reference(tab_words, tab_scales, ws_words, ws_scales, wt_words, wt_scales, sm, wd, wgo, offs, offs2):
    idx = unstriped(offs)
    idx2 = unstriped(offs2)
    tab_ = unpack_weight(tab_words, tab_scales, "e4m3")[:, idx]
    tabb_ = unpack_weight(tab_words, tab_scales, "e4m3")[:, idx2]
    ws_ = unpack_weight(ws_words, ws_scales, "e4m3")
    wt_ = unpack_weight(wt_words, wt_scales, "e4m3")
    a = ws_.T @ tab_ + wt_.T @ tabb_
    h = f64(sm)[:, None] * silu(a)
    h_ = mxq(h, 0, "e4m3")
    wd_ = mxq(f64(wd), 0, "e4m3")
    y = wd_.T @ h_
    out = np.zeros((N, T))
    out[:, idx2] = f64(wgo)[0] * (y)
    return out

@@ -1,0 +1,221 @@
+from contextlib import ExitStack
+
+import concourse.mybir as mybir
+from concourse.masks import make_identity
+
+K, R, N, T, J = 512, 512, 512, 2048, 1024
+FLOPS = 2 * (2 * K * R * J + R * N * J)
+
+F32 = mybir.dt.float32
+BF16 = mybir.dt.bfloat16
+I32 = mybir.dt.int32
+U32 = mybir.dt.uint32
+U16 = mybir.dt.uint16
+U8 = mybir.dt.uint8
+FP8X4 = mybir.dt.float8_e4m3fn_x4
+ACT = mybir.ActivationFunctionType
+MULT = mybir.AluOpType.mult
+
+P = 128
+PACK = 4
+QUARTER = J // 4
+
+
+def tile_list_msg_silu_none_kernel(
+    tc, tab_words, tab_scales, ws_words, ws_scales, wt_words, wt_scales, sm, wd, wgo, offs, offs2, out
+):
+    nc = tc.nc
+    with ExitStack() as ctx:
+        keep = ctx.enter_context(tc.tile_pool(name="keep", bufs=1))
+        ring = ctx.enter_context(tc.tile_pool(name="ring", bufs=2))
+        psum = ctx.enter_context(tc.psum_pool(name="psum", bufs=2))
+
+        src_list = keep.tile([P, J // 16], U16, name="src_list")
+        dst_list = keep.tile([P, J // 16], U16, name="dst_list")
+        nc.sync.dma_start(src_list[:], offs)
+
+        tab_plane = keep.tile([P, T // 4], I32, name="tab_plane", align_bytes=64)
+        w_planes = keep.tile([P, 2, R // 4], I32, name="w_planes", align_bytes=64)
+        nc.vector.memset(tab_plane[:], 0)
+        nc.vector.memset(w_planes[:], 0)
+
+        def scale_rows(scales, r):
+            return scales[0].rearrange("(q r) t -> r q t", r=4)[r].bitcast(I32)
+
+        for r in range(4):
+            nc.sync.dma_start(tab_plane[r:P:32, :], scale_rows(tab_scales, r))
+        nc.sync.dma_start(dst_list[:], offs2)
+
+        def words(packed):
+            return packed[0].rearrange("p c i -> p (c i)").bitcast(I32)
+
+        tab = keep.tile([P, T], I32, name="tab", tag="tab_then_window", align_bytes=64)
+        w_words = keep.tile([P, 2, R], I32, name="w_words", align_bytes=64)
+        wd_raw = keep.tile([P, 2, PACK, N // 2], F32, name="wd_raw", tag="wd_then_window", align_bytes=64)
+        wgo_sb = keep.tile([P, J], F32, name="wgo_sb")
+        sm_sb = keep.tile([P, PACK], F32, name="sm_sb")
+        wd_rows = wd.rearrange("(p t) n -> p t n", t=PACK)
+        nc.gpsimd.dma_start(tab[:], words(tab_words))
+        for r in range(4):
+            nc.sync.dma_start(w_planes[r:P:32, 0, :], scale_rows(ws_scales, r))
+        for r in range(4):
+            nc.sync.dma_start(w_planes[r:P:32, 1, :], scale_rows(wt_scales, r))
+        nc.sync.dma_start(w_words[:, 0, :], words(ws_words))
+        nc.sync.dma_start(w_words[:, 1, :], words(wt_words))
+        nc.sync.dma_start(sm_sb[:], sm.rearrange("(p t) -> p t", t=PACK))
+        nc.sync.dma_start(wd_raw[:, 0], wd_rows[:, :, 0 : N // 2])
+        nc.sync.dma_start(wgo_sb[:], wgo)
+        nc.sync.dma_start(wd_raw[:, 1], wd_rows[:, :, N // 2 : N])
+
+        ident = keep.tile([P, P], F32, name="ident")
+        make_identity(nc, ident[:])
+        windows = {}
+        for n in range(2):
+            windows[n] = keep.tile([P, T], F32, name="window%d" % n)
+            nc.gpsimd.memset(windows[n][:], 0.0)
+
+        lists = (src_list, dst_list)
+        v_words = [keep.tile([P, J], U32, name="v_words%d" % s, align_bytes=64) for s in range(2)]
+        v_scales = [keep.tile([P, J], U8, name="v_scales%d" % s, align_bytes=64) for s in range(2)]
+        wd_bf = keep.tile([P, N, PACK], BF16, name="wd_bf", align_bytes=64)
+        wd_codes = keep.tile([P, N], U32, name="wd_codes", align_bytes=64)
+        wd_scales = keep.tile([P, N], U8, name="wd_scales", align_bytes=64)
+        h_codes = keep.tile([P, J], U32, name="h_codes", align_bytes=64)
+        h_scales = keep.tile([P, J], U8, name="h_scales", align_bytes=64)
+        y = [keep.tile([P, J], F32, name="y%d" % n) for n in range(4)]
+        h_grouped = {}
+
+        def offsets(lst, j0, j1):
+            return lst[:, j0 // 16 : j1 // 16]
+
+        def gather_scales(s, j0, j1):
+            nc.vector.tensor_copy(v_scales[s][:, j0:j1], tab_plane[:].bitcast(U8).indirect(offsets(lists[s], j0, j1)))
+
+        def gather_words(s, j0, j1):
+            nc.vector.tensor_copy(v_words[s][:, j0:j1], tab[:].bitcast(U32).indirect(offsets(lists[s], j0, j1)))
+
+        def hidden(q):
+            h_planes = ring.tile([P, PACK, QUARTER], BF16, name="h_planes")
+            for half in range(2):
+                cols = slice(q * QUARTER + half * P, q * QUARTER + (half + 1) * P)
+                a_ps = psum.tile([P, R], F32, name="a_ps")
+                for s in range(2):
+                    nc.tensor.matmul_mx(
+                        out=a_ps[:],
+                        lhsT=v_words[s][:, cols].bitcast(FP8X4),
+                        lhsT_scale=v_scales[s][:, cols],
+                        rhs=w_words[:, s, :].bitcast(FP8X4),
+                        rhs_scale=w_planes[:, s, :].bitcast(U8),
+                        start=(s == 0),
+                        stop=(s == 1),
+                    )
+                act = ring.tile([P, PACK, P], F32, name="act")
+                nc.scalar.activation(act[:], a_ps[:].rearrange("j (p t) -> j t p", t=PACK), ACT.Silu)
+                act_t = psum.tile([P, PACK, P], F32, name="act_t")
+                for t in range(PACK):
+                    nc.tensor.transpose(act_t[:, t, :], act[:, t, :], ident[:])
+                for t in range(PACK):
+                    nc.scalar.activation(
+                        h_planes[:, t, half * P : (half + 1) * P], act_t[:, t, :], ACT.Copy, scale=sm_sb[:, t : t + 1]
+                    )
+            h_grouped[q] = ring.tile([P, QUARTER, PACK], BF16, name="h_grouped", align_bytes=64)
+            nc.scalar.copy(
+                h_grouped[q][:].rearrange("p (c i) t -> p c t i", i=4),
+                h_planes[:].rearrange("p t (c i) -> p c t i", i=4),
+            )
+
+        def quantise_hidden(q):
+            cols = slice(q * QUARTER, (q + 1) * QUARTER)
+            nc.vector.quantize_mx(
+                out=h_codes[:, cols].bitcast(FP8X4),
+                scales=h_scales[:, cols],
+                in_=h_grouped[q][:].rearrange("p j t -> p (j t)"),
+            )
+
+        def cast_wd(half, copy):
+            cols = slice(half * (N // 2), (half + 1) * (N // 2))
+            copy(
+                wd_bf[:, cols, :].rearrange("p (c i) t -> p c t i", i=4),
+                wd_raw[:, half].rearrange("p t (c i) -> p c t i", i=4),
+            )
+
+        def quantise_wd(half):
+            cols = slice(half * (N // 2), (half + 1) * (N // 2))
+            nc.vector.quantize_mx(
+                out=wd_codes[:, cols].bitcast(FP8X4),
+                scales=wd_scales[:, cols],
+                in_=wd_bf[:, cols, :].rearrange("p n t -> p (n t)"),
+            )
+
+        def message(n_tiles, j0, j1):
+            width = j1 - j0
+            y_ps = psum.tile([P, 512], F32, name="y_ps", bufs=4)
+            for i, n in enumerate(n_tiles):
+                nc.tensor.matmul_mx(
+                    out=y_ps[:, i * width : (i + 1) * width],
+                    lhsT=wd_codes[:, n * P : (n + 1) * P].bitcast(FP8X4),
+                    lhsT_scale=wd_scales[:, n * P : (n + 1) * P],
+                    rhs=h_codes[:, j0:j1].bitcast(FP8X4),
+                    rhs_scale=h_scales[:, j0:j1],
+                    start=True,
+                    stop=True,
+                )
+            for i, n in enumerate(n_tiles):
+                nc.scalar.copy(y[n][:, j0:j1], y_ps[:, i * width : (i + 1) * width])
+
+        def scatter(n, j0, j1):
+            nc.vector.tensor_tensor(
+                windows[n][:].indirect(offsets(dst_list, j0, j1)), y[n][:, j0:j1], wgo_sb[:, j0:j1], MULT
+            )
+
+        def store(n):
+            nc.sync.dma_start(out[n * P : (n + 1) * P, :], windows[n][:])
+
+        q0, q1, q2, q3, q4 = range(0, J + 1, QUARTER)
+        for j0, j1 in ((q0, q1), (q1, q2)):
+            for s in range(2):
+                gather_scales(s, j0, j1)
+            for s in range(2):
+                gather_words(s, j0, j1)
+        hidden(0)
+        gather_scales(0, q2, q4)
+        gather_scales(1, q2, q4)
+        gather_words(0, q2, q4)
+        cast_wd(0, nc.vector.tensor_copy)
+        gather_words(1, q2, q4)
+        quantise_wd(0)
+        windows[2] = keep.tile([P, T], F32, name="window2", tag="tab_then_window", align_bytes=64)
+        nc.gpsimd.memset(windows[2][:], 0.0)
+
+        quantise_hidden(0)
+        message((0, 1), q0, q1)
+        hidden(1)
+        quantise_hidden(1)
+        message((0, 1), q1, q2)
+        cast_wd(1, nc.scalar.copy)
+        quantise_wd(1)
+        windows[3] = keep.tile([P, T], F32, name="window3", tag="wd_then_window", align_bytes=64)
+        nc.gpsimd.memset(windows[3][:], 0.0)
+        message((2,), q0, q2)
+        hidden(2)
+        quantise_hidden(2)
+        message((0, 1), q2, q3)
+        hidden(3)
+        quantise_hidden(3)
+        message((0, 1), q3, q4)
+        message((3,), q0, q2)
+        message((2,), q2, q4)
+        message((3,), q2, q4)
+
+        for j0, j1 in ((q0, q1), (q1, q2), (q2, q3), (q3, q4)):
+            scatter(0, j0, j1)
+            if j1 == q4:
+                store(0)
+            scatter(1, j0, j1)
+        store(1)
+        scatter(2, q0, q2)
+        scatter(2, q2, q4)
+        store(2)
+        scatter(3, q0, q2)
+        scatter(3, q2, q4)
+        store(3)

@@ -33,25 +33,26 @@ def tile_list_msg_silu_none_kernel(
         src_list = keep.tile([P, J // 16], U16, name="src_list")
         dst_list = keep.tile([P, J // 16], U16, name="dst_list")
         nc.sync.dma_start(src_list[:], offs)
+        nc.sync.dma_start(dst_list[:], offs2)
 
         tab_plane = keep.tile([P, T // 4], I32, name="tab_plane", align_bytes=64)
         w_planes = keep.tile([P, 2, R // 4], I32, name="w_planes", align_bytes=64)
         nc.vector.memset(tab_plane[:], 0)
-        nc.vector.memset(w_planes[:], 0)
+        nc.gpsimd.memset(w_planes[:], 0)
 
         def scale_rows(scales, r):
             return scales[0].rearrange("(q r) t -> r q t", r=4)[r].bitcast(I32)
 
         for r in range(4):
-            nc.sync.dma_start(tab_plane[r:P:32, :], scale_rows(tab_scales, r))
-        nc.sync.dma_start(dst_list[:], offs2)
+            queue = nc.sync if r == 0 else nc.scalar
+            queue.dma_start(tab_plane[r:P:32, :], scale_rows(tab_scales, r))
 
         def words(packed):
             return packed[0].rearrange("p c i -> p (c i)").bitcast(I32)
 
-        tab = keep.tile([P, T], I32, name="tab", tag="tab_then_window", align_bytes=64)
+        tab = keep.tile([P, T], I32, name="tab", align_bytes=64)
         w_words = keep.tile([P, 2, R], I32, name="w_words", align_bytes=64)
-        wd_raw = keep.tile([P, 2, PACK, N // 2], F32, name="wd_raw", tag="wd_then_window", align_bytes=64)
+        wd_raw = keep.tile([P, 2, PACK, N // 2], F32, name="wd_raw")
         wgo_sb = keep.tile([P, J], F32, name="wgo_sb")
         sm_sb = keep.tile([P, PACK], F32, name="sm_sb")
         wd_rows = wd.rearrange("(p t) n -> p t n", t=PACK)
@@ -59,7 +60,7 @@ def tile_list_msg_silu_none_kernel(
         for r in range(4):
             nc.sync.dma_start(w_planes[r:P:32, 0, :], scale_rows(ws_scales, r))
         for r in range(4):
-            nc.sync.dma_start(w_planes[r:P:32, 1, :], scale_rows(wt_scales, r))
+            nc.scalar.dma_start(w_planes[r:P:32, 1, :], scale_rows(wt_scales, r))
         nc.sync.dma_start(w_words[:, 0, :], words(ws_words))
         nc.sync.dma_start(w_words[:, 1, :], words(wt_words))
         nc.sync.dma_start(sm_sb[:], sm.rearrange("(p t) -> p t", t=PACK))
@@ -70,20 +71,20 @@ def tile_list_msg_silu_none_kernel(
         ident = keep.tile([P, P], F32, name="ident")
         make_identity(nc, ident[:])
         windows = {}
-        for n in range(2):
+        for n in range(3):
             windows[n] = keep.tile([P, T], F32, name="window%d" % n)
             nc.gpsimd.memset(windows[n][:], 0.0)
 
         lists = (src_list, dst_list)
         v_words = [keep.tile([P, J], U32, name="v_words%d" % s, align_bytes=64) for s in range(2)]
         v_scales = [keep.tile([P, J], U8, name="v_scales%d" % s, align_bytes=64) for s in range(2)]
-        wd_bf = keep.tile([P, N, PACK], BF16, name="wd_bf", align_bytes=64)
         wd_codes = keep.tile([P, N], U32, name="wd_codes", align_bytes=64)
         wd_scales = keep.tile([P, N], U8, name="wd_scales", align_bytes=64)
         h_codes = keep.tile([P, J], U32, name="h_codes", align_bytes=64)
         h_scales = keep.tile([P, J], U8, name="h_scales", align_bytes=64)
-        y = [keep.tile([P, J], F32, name="y%d" % n) for n in range(4)]
         h_grouped = {}
+        wd_bf = {}
+        y = {}
 
         def offsets(lst, j0, j1):
             return lst[:, j0 // 16 : j1 // 16]
@@ -95,10 +96,10 @@ def tile_list_msg_silu_none_kernel(
             nc.vector.tensor_copy(v_words[s][:, j0:j1], tab[:].bitcast(U32).indirect(offsets(lists[s], j0, j1)))
 
         def hidden(q):
-            h_planes = ring.tile([P, PACK, QUARTER], BF16, name="h_planes")
+            h_planes = keep.tile([P, PACK, QUARTER], BF16, name="h_planes%d" % q, tag="planes%d" % q)
             for half in range(2):
                 cols = slice(q * QUARTER + half * P, q * QUARTER + (half + 1) * P)
-                a_ps = psum.tile([P, R], F32, name="a_ps")
+                a_ps = psum.tile([P, R], F32, name="a_ps", tag="bank%d" % (2 * (q % 2) + half), bufs=1)
                 for s in range(2):
                     nc.tensor.matmul_mx(
                         out=a_ps[:],
@@ -111,14 +112,14 @@ def tile_list_msg_silu_none_kernel(
                     )
                 act = ring.tile([P, PACK, P], F32, name="act")
                 nc.scalar.activation(act[:], a_ps[:].rearrange("j (p t) -> j t p", t=PACK), ACT.Silu)
-                act_t = psum.tile([P, PACK, P], F32, name="act_t")
+                act_t = psum.tile([P, PACK, P], F32, name="act_t", tag="bank%d" % (2 * (1 - q % 2) + half), bufs=1)
                 for t in range(PACK):
                     nc.tensor.transpose(act_t[:, t, :], act[:, t, :], ident[:])
                 for t in range(PACK):
                     nc.scalar.activation(
                         h_planes[:, t, half * P : (half + 1) * P], act_t[:, t, :], ACT.Copy, scale=sm_sb[:, t : t + 1]
                     )
-            h_grouped[q] = ring.tile([P, QUARTER, PACK], BF16, name="h_grouped", align_bytes=64)
+            h_grouped[q] = keep.tile([P, QUARTER, PACK], BF16, name="h_grouped%d" % q, tag="grouped%d" % q, align_bytes=64)
             nc.scalar.copy(
                 h_grouped[q][:].rearrange("p (c i) t -> p c t i", i=4),
                 h_planes[:].rearrange("p t (c i) -> p c t i", i=4),
@@ -132,10 +133,10 @@ def tile_list_msg_silu_none_kernel(
                 in_=h_grouped[q][:].rearrange("p j t -> p (j t)"),
             )
 
-        def cast_wd(half, copy):
-            cols = slice(half * (N // 2), (half + 1) * (N // 2))
-            copy(
-                wd_bf[:, cols, :].rearrange("p (c i) t -> p c t i", i=4),
+        def cast_wd(half, tag):
+            wd_bf[half] = keep.tile([P, N // 2, PACK], BF16, name="wd_bf%d" % half, tag=tag, align_bytes=64)
+            nc.vector.tensor_copy(
+                wd_bf[half][:].rearrange("p (c i) t -> p c t i", i=4),
                 wd_raw[:, half].rearrange("p t (c i) -> p c t i", i=4),
             )
 
@@ -144,15 +145,19 @@ def tile_list_msg_silu_none_kernel(
             nc.vector.quantize_mx(
                 out=wd_codes[:, cols].bitcast(FP8X4),
                 scales=wd_scales[:, cols],
-                in_=wd_bf[:, cols, :].rearrange("p n t -> p (n t)"),
+                in_=wd_bf[half][:].rearrange("p n t -> p (n t)"),
             )
 
-        def message(n_tiles, j0, j1):
-            width = j1 - j0
-            y_ps = psum.tile([P, 512], F32, name="y_ps", bufs=4)
-            for i, n in enumerate(n_tiles):
+        def message(pieces, bank, bank_bufs, tag, one_copy=True):
+            y_ps = psum.tile([P, 512], F32, name=bank, bufs=bank_bufs)
+            y_sb = keep.tile([P, 512], F32, name="y_%d_%d" % pieces[0][:2], tag=tag)
+            spans = []
+            for n, j0, j1 in pieces:
+                at = spans[-1].stop if spans else 0
+                spans.append(slice(at, at + j1 - j0))
+                y[n, j0] = y_sb[:, spans[-1]]
                 nc.tensor.matmul_mx(
-                    out=y_ps[:, i * width : (i + 1) * width],
+                    out=y_ps[:, spans[-1]],
                     lhsT=wd_codes[:, n * P : (n + 1) * P].bitcast(FP8X4),
                     lhsT_scale=wd_scales[:, n * P : (n + 1) * P],
                     rhs=h_codes[:, j0:j1].bitcast(FP8X4),
@@ -160,62 +165,72 @@ def tile_list_msg_silu_none_kernel(
                     start=True,
                     stop=True,
                 )
-            for i, n in enumerate(n_tiles):
-                nc.scalar.copy(y[n][:, j0:j1], y_ps[:, i * width : (i + 1) * width])
+            for span in [slice(0, spans[-1].stop)] if one_copy else spans:
+                nc.scalar.copy(y_sb[:, span], y_ps[:, span])
 
         def scatter(n, j0, j1):
-            nc.vector.tensor_tensor(
-                windows[n][:].indirect(offsets(dst_list, j0, j1)), y[n][:, j0:j1], wgo_sb[:, j0:j1], MULT
-            )
+            nc.vector.tensor_tensor(windows[n][:].indirect(offsets(dst_list, j0, j1)), y[n, j0], wgo_sb[:, j0:j1], MULT)
 
         def store(n):
             nc.sync.dma_start(out[n * P : (n + 1) * P, :], windows[n][:])
 
         q0, q1, q2, q3, q4 = range(0, J + 1, QUARTER)
-        for j0, j1 in ((q0, q1), (q1, q2)):
-            for s in range(2):
-                gather_scales(s, j0, j1)
-            for s in range(2):
-                gather_words(s, j0, j1)
-        hidden(0)
-        gather_scales(0, q2, q4)
+        gather_scales(0, q0, q1)
+        gather_scales(1, q0, q1)
+        gather_scales(0, q1, q2)
+        gather_scales(1, q1, q2)
+        gather_scales(0, q2, q3)
+        gather_words(0, q0, q1)
+        gather_words(1, q0, q1)
+        gather_words(0, q1, q2)
+        gather_words(1, q1, q2)
+        gather_scales(0, q3, q4)
         gather_scales(1, q2, q4)
         gather_words(0, q2, q4)
-        cast_wd(0, nc.vector.tensor_copy)
+        cast_wd(0, "wd_bf0")
         gather_words(1, q2, q4)
         quantise_wd(0)
-        windows[2] = keep.tile([P, T], F32, name="window2", tag="tab_then_window", align_bytes=64)
-        nc.gpsimd.memset(windows[2][:], 0.0)
 
+        hidden(0)
         quantise_hidden(0)
-        message((0, 1), q0, q1)
+        message([(0, q0, q1), (1, q0, q1)], "y_ps", 2, "y01_0", one_copy=False)
+        cast_wd(1, "grouped0")
+        quantise_wd(1)
+        scatter(0, q0, q1)
+        scatter(1, q0, q1)
+
         hidden(1)
         quantise_hidden(1)
-        message((0, 1), q1, q2)
-        cast_wd(1, nc.scalar.copy)
-        quantise_wd(1)
-        windows[3] = keep.tile([P, T], F32, name="window3", tag="wd_then_window", align_bytes=64)
+        windows[3] = keep.tile([P, T], F32, name="window3", tag="grouped1", align_bytes=64)
         nc.gpsimd.memset(windows[3][:], 0.0)
-        message((2,), q0, q2)
+        message([(2, q0, q1)], "y2_ps", 1, "planes1")
+        message([(0, q1, q2), (1, q1, q2)], "y_ps", 2, "y01_1")
+        scatter(2, q0, q1)
+        scatter(0, q1, q2)
+        scatter(1, q1, q2)
+
         hidden(2)
         quantise_hidden(2)
-        message((0, 1), q2, q3)
+        message([(2, q1, q2)], "y2_ps", 1, "planes2")
+        message([(0, q2, q3), (1, q2, q3)], "y_ps", 2, "y01_2")
+        scatter(2, q1, q2)
+        scatter(0, q2, q3)
+        scatter(1, q2, q3)
+
         hidden(3)
         quantise_hidden(3)
-        message((0, 1), q3, q4)
-        message((3,), q0, q2)
-        message((2,), q2, q4)
-        message((3,), q2, q4)
-
-        for j0, j1 in ((q0, q1), (q1, q2), (q2, q3), (q3, q4)):
-            scatter(0, j0, j1)
-            if j1 == q4:
-                store(0)
-            scatter(1, j0, j1)
+        message([(2, q2, q3), (3, q0, q1)], "y2_ps", 1, "planes3")
+        message([(0, q3, q4), (1, q3, q4)], "y_ps", 2, "y01_3")
+        message([(2, q3, q4), (3, q3, q4)], "y_ps", 2, "y23_3")
+        message([(3, q1, q3)], "y3_ps", 1, "y01_3")
+        scatter(2, q2, q3)
+        scatter(3, q0, q1)
+        scatter(0, q3, q4)
+        store(0)
+        scatter(1, q3, q4)
         store(1)
-        scatter(2, q0, q2)
-        scatter(2, q2, q4)
+        scatter(2, q3, q4)
         store(2)
-        scatter(3, q0, q2)
-        scatter(3, q2, q4)
+        scatter(3, q3, q4)
+        scatter(3, q1, q3)
         store(3)

@@ -19,6 +19,9 @@ MULT = mybir.AluOpType.mult
 P = 128
 PACK = 4
 QUARTER = J // 4
+AT_PLANES0 = 0
+AT_WD_RAW = 10240
+AT_FIRST_WORDS = 18432
 
 
 def tile_list_msg_silu_none_kernel(
@@ -27,8 +30,12 @@ def tile_list_msg_silu_none_kernel(
     nc = tc.nc
     with ExitStack() as ctx:
         keep = ctx.enter_context(tc.tile_pool(name="keep", bufs=1))
+        reuse = ctx.enter_context(tc.tile_pool(name="reuse", bufs=1))
         ring = ctx.enter_context(tc.tile_pool(name="ring", bufs=2))
-        psum = ctx.enter_context(tc.psum_pool(name="psum", bufs=2))
+        psum = ctx.enter_context(tc.psum_pool(name="psum", bufs=1))
+
+        def placed(shape, dtype, name, offset):
+            return reuse.tile(shape, dtype, name=name, offset=offset, align_bytes=64)
 
         src_list = keep.tile([P, J // 16], U16, name="src_list")
         dst_list = keep.tile([P, J // 16], U16, name="dst_list")
@@ -36,93 +43,124 @@ def tile_list_msg_silu_none_kernel(
         nc.sync.dma_start(dst_list[:], offs2)
 
         tab_plane = keep.tile([P, T // 4], I32, name="tab_plane", align_bytes=64)
-        w_planes = keep.tile([P, 2, R // 4], I32, name="w_planes", align_bytes=64)
+        w_planes = [keep.tile([P, R // 4], I32, name="w_plane%d" % s, align_bytes=64) for s in range(2)]
+        ident = keep.tile([P, P], F32, name="ident")
         nc.vector.memset(tab_plane[:], 0)
-        nc.gpsimd.memset(w_planes[:], 0)
+        nc.gpsimd.memset(w_planes[0][:], 0)
+        nc.gpsimd.memset(ident[:], 0.0)
+        nc.gpsimd.memset(w_planes[1][:], 0)
+        make_identity(nc, ident[:], nomemset=True)
 
         def scale_rows(scales, r):
             return scales[0].rearrange("(q r) t -> r q t", r=4)[r].bitcast(I32)
-
-        for r in range(4):
-            queue = nc.sync if r == 0 else nc.scalar
-            queue.dma_start(tab_plane[r:P:32, :], scale_rows(tab_scales, r))
 
         def words(packed):
             return packed[0].rearrange("p c i -> p (c i)").bitcast(I32)
 
         tab = keep.tile([P, T], I32, name="tab", align_bytes=64)
-        w_words = keep.tile([P, 2, R], I32, name="w_words", align_bytes=64)
-        wd_raw = keep.tile([P, 2, PACK, N // 2], F32, name="wd_raw")
+        w_words = [keep.tile([P, R], I32, name="w_words%d" % s, align_bytes=64) for s in range(2)]
+        wd_raw = placed([P, PACK, N], F32, "wd_raw", AT_WD_RAW)
         wgo_sb = keep.tile([P, J], F32, name="wgo_sb")
         sm_sb = keep.tile([P, PACK], F32, name="sm_sb")
-        wd_rows = wd.rearrange("(p t) n -> p t n", t=PACK)
-        nc.gpsimd.dma_start(tab[:], words(tab_words))
         for r in range(4):
-            nc.sync.dma_start(w_planes[r:P:32, 0, :], scale_rows(ws_scales, r))
+            queue = nc.sync if r < 2 else nc.scalar
+            queue.dma_start(tab_plane[r:P:32, :], scale_rows(tab_scales, r))
+        nc.sync.dma_start(w_planes[0][0:P:32, :], scale_rows(ws_scales, 0))
+        nc.sync.dma_start(tab[:], words(tab_words))
+        for r in range(1, 4):
+            nc.sync.dma_start(w_planes[0][r:P:32, :], scale_rows(ws_scales, r))
+        nc.sync.dma_start(w_words[0][:], words(ws_words))
         for r in range(4):
-            nc.scalar.dma_start(w_planes[r:P:32, 1, :], scale_rows(wt_scales, r))
-        nc.sync.dma_start(w_words[:, 0, :], words(ws_words))
-        nc.sync.dma_start(w_words[:, 1, :], words(wt_words))
+            queue = nc.sync if r < 2 else nc.gpsimd
+            queue.dma_start(w_planes[1][r:P:32, :], scale_rows(wt_scales, r))
+        nc.sync.dma_start(w_words[1][:], words(wt_words))
         nc.sync.dma_start(sm_sb[:], sm.rearrange("(p t) -> p t", t=PACK))
-        nc.sync.dma_start(wd_raw[:, 0], wd_rows[:, :, 0 : N // 2])
+        nc.sync.dma_start(wd_raw[:], wd.rearrange("(p t) n -> p t n", t=PACK))
         nc.sync.dma_start(wgo_sb[:], wgo)
-        nc.sync.dma_start(wd_raw[:, 1], wd_rows[:, :, N // 2 : N])
 
-        ident = keep.tile([P, P], F32, name="ident")
-        make_identity(nc, ident[:])
         windows = {}
         for n in range(3):
             windows[n] = keep.tile([P, T], F32, name="window%d" % n)
             nc.gpsimd.memset(windows[n][:], 0.0)
 
         lists = (src_list, dst_list)
-        v_words = [keep.tile([P, J], U32, name="v_words%d" % s, align_bytes=64) for s in range(2)]
-        v_scales = [keep.tile([P, J], U8, name="v_scales%d" % s, align_bytes=64) for s in range(2)]
-        wd_codes = keep.tile([P, N], U32, name="wd_codes", align_bytes=64)
-        wd_scales = keep.tile([P, N], U8, name="wd_scales", align_bytes=64)
+        v_words = {}
+        v_scales = {}
+        wd_bf = {}
+        wd_mx = {}
         h_codes = keep.tile([P, J], U32, name="h_codes", align_bytes=64)
         h_scales = keep.tile([P, J], U8, name="h_scales", align_bytes=64)
         h_grouped = {}
-        wd_bf = {}
         y = {}
 
         def offsets(lst, j0, j1):
             return lst[:, j0 // 16 : j1 // 16]
 
-        def gather_scales(s, j0, j1):
-            nc.vector.tensor_copy(v_scales[s][:, j0:j1], tab_plane[:].bitcast(U8).indirect(offsets(lists[s], j0, j1)))
+        def fresh(shape, dtype, name, offset):
+            if offset is None:
+                return keep.tile(shape, dtype, name=name, align_bytes=64)
+            return placed(shape, dtype, name, offset)
 
-        def gather_words(s, j0, j1):
-            nc.vector.tensor_copy(v_words[s][:, j0:j1], tab[:].bitcast(U32).indirect(offsets(lists[s], j0, j1)))
+        def gather(picked, window, dtype, name, s, j0, j1, offset):
+            tile = fresh([P, j1 - j0], dtype, "%s%d_%d" % (name, s, j0), offset)
+            nc.vector.tensor_copy(tile[:], window[:].bitcast(dtype).indirect(offsets(lists[s], j0, j1)))
+            for j in range(j0, j1, P):
+                picked[s, j] = tile[:, j - j0 : j - j0 + P]
 
-        def hidden(q):
-            h_planes = keep.tile([P, PACK, QUARTER], BF16, name="h_planes%d" % q, tag="planes%d" % q)
-            for half in range(2):
-                cols = slice(q * QUARTER + half * P, q * QUARTER + (half + 1) * P)
-                a_ps = psum.tile([P, R], F32, name="a_ps", tag="bank%d" % (2 * (q % 2) + half), bufs=1)
-                for s in range(2):
-                    nc.tensor.matmul_mx(
-                        out=a_ps[:],
-                        lhsT=v_words[s][:, cols].bitcast(FP8X4),
-                        lhsT_scale=v_scales[s][:, cols],
-                        rhs=w_words[:, s, :].bitcast(FP8X4),
-                        rhs_scale=w_planes[:, s, :].bitcast(U8),
-                        start=(s == 0),
-                        stop=(s == 1),
-                    )
-                act = ring.tile([P, PACK, P], F32, name="act")
-                nc.scalar.activation(act[:], a_ps[:].rearrange("j (p t) -> j t p", t=PACK), ACT.Silu)
-                act_t = psum.tile([P, PACK, P], F32, name="act_t", tag="bank%d" % (2 * (1 - q % 2) + half), bufs=1)
-                for t in range(PACK):
-                    nc.tensor.transpose(act_t[:, t, :], act[:, t, :], ident[:])
-                for t in range(PACK):
-                    nc.scalar.activation(
-                        h_planes[:, t, half * P : (half + 1) * P], act_t[:, t, :], ACT.Copy, scale=sm_sb[:, t : t + 1]
-                    )
+        def gather_scales(s, j0, j1, offset=None):
+            gather(v_scales, tab_plane, U8, "v_scales", s, j0, j1, offset)
+
+        def gather_words(s, j0, j1, offset=None):
+            gather(v_words, tab, U32, "v_words", s, j0, j1, offset)
+
+        a_ps = {}
+        act = {}
+        act_t = {}
+        h_planes = {}
+
+        def project(q, half, s):
+            j = q * QUARTER + half * P
+            if s == 0:
+                a_ps[j] = psum.tile([P, R], F32, name="a_ps", tag="bank%d" % (2 * (q % 2) + half))
+            nc.tensor.matmul_mx(
+                out=a_ps[j][:],
+                lhsT=v_words[s, j].bitcast(FP8X4),
+                lhsT_scale=v_scales[s, j],
+                rhs=w_words[s][:].bitcast(FP8X4),
+                rhs_scale=w_planes[s][:].bitcast(U8),
+                start=(s == 0),
+                stop=(s == 1),
+            )
+
+        def activate(q, half):
+            j = q * QUARTER + half * P
+            act[j] = ring.tile([P, PACK, P], F32, name="act")
+            act_t[j] = psum.tile([P, PACK, P], F32, name="act_t", tag="bank%d" % (2 * (1 - q % 2) + half))
+            step = 2 if j == 0 else PACK
+            for t0 in range(0, PACK, step):
+                planes = slice(t0, t0 + step)
+                nc.scalar.activation(
+                    act[j][:, planes, :], a_ps[j][:].rearrange("j (p t) -> j t p", t=PACK)[:, planes, :], ACT.Silu
+                )
+                for t in range(t0, t0 + step):
+                    nc.tensor.transpose(act_t[j][:, t, :], act[j][:, t, :], ident[:])
+
+        def smooth(q, half):
+            j = q * QUARTER + half * P
+            if half == 0 and q == 0:
+                h_planes[q] = placed([P, PACK, QUARTER], BF16, "h_planes0", AT_PLANES0)
+            elif half == 0:
+                h_planes[q] = keep.tile([P, PACK, QUARTER], BF16, name="h_planes", tag="planes%d" % q)
+            for t in range(PACK):
+                nc.scalar.activation(
+                    h_planes[q][:, t, half * P : (half + 1) * P], act_t[j][:, t, :], ACT.Copy, scale=sm_sb[:, t : t + 1]
+                )
+
+        def interleave(q):
             h_grouped[q] = keep.tile([P, QUARTER, PACK], BF16, name="h_grouped%d" % q, tag="grouped%d" % q, align_bytes=64)
             nc.scalar.copy(
                 h_grouped[q][:].rearrange("p (c i) t -> p c t i", i=4),
-                h_planes[:].rearrange("p t (c i) -> p c t i", i=4),
+                h_planes[q][:].rearrange("p t (c i) -> p c t i", i=4),
             )
 
         def quantise_hidden(q):
@@ -133,43 +171,50 @@ def tile_list_msg_silu_none_kernel(
                 in_=h_grouped[q][:].rearrange("p j t -> p (j t)"),
             )
 
-        def cast_wd(half, tag):
-            wd_bf[half] = keep.tile([P, N // 2, PACK], BF16, name="wd_bf%d" % half, tag=tag, align_bytes=64)
-            nc.vector.tensor_copy(
-                wd_bf[half][:].rearrange("p (c i) t -> p c t i", i=4),
-                wd_raw[:, half].rearrange("p t (c i) -> p c t i", i=4),
+        def cast_wd(copy, n0, n1, offset=None):
+            wd_bf[n0] = fresh([P, (n1 - n0) * P, PACK], BF16, "wd_bf%d" % n0, offset)
+            copy(
+                wd_bf[n0][:].rearrange("p (c i) t -> p c t i", i=4),
+                wd_raw[:, :, n0 * P : n1 * P].rearrange("p t (c i) -> p c t i", i=4),
             )
 
-        def quantise_wd(half):
-            cols = slice(half * (N // 2), (half + 1) * (N // 2))
+        def quantise_wd(n0, n1, offset=None):
+            codes = fresh([P, (n1 - n0) * P], U32, "wd_codes%d" % n0, offset)
+            scales = keep.tile([P, (n1 - n0) * P], U8, name="wd_scales%d" % n0, align_bytes=64)
             nc.vector.quantize_mx(
-                out=wd_codes[:, cols].bitcast(FP8X4),
-                scales=wd_scales[:, cols],
-                in_=wd_bf[half][:].rearrange("p n t -> p (n t)"),
+                out=codes[:].bitcast(FP8X4), scales=scales[:], in_=wd_bf[n0][:].rearrange("p n t -> p (n t)")
             )
+            for n in range(n0, n1):
+                cols = slice((n - n0) * P, (n - n0 + 1) * P)
+                wd_mx[n] = (codes[:, cols], scales[:, cols])
 
-        def message(pieces, bank, bank_bufs, tag, one_copy=True):
-            y_ps = psum.tile([P, 512], F32, name=bank, bufs=bank_bufs)
-            y_sb = keep.tile([P, 512], F32, name="y_%d_%d" % pieces[0][:2], tag=tag)
-            spans = []
+        y_ps = {}
+
+        def message(pieces, bank):
+            tile = psum.tile([P, 512], F32, name="y_ps", tag=bank)
+            at = 0
             for n, j0, j1 in pieces:
-                at = spans[-1].stop if spans else 0
-                spans.append(slice(at, at + j1 - j0))
-                y[n, j0] = y_sb[:, spans[-1]]
+                y_ps[n, j0] = (tile, at)
                 nc.tensor.matmul_mx(
-                    out=y_ps[:, spans[-1]],
-                    lhsT=wd_codes[:, n * P : (n + 1) * P].bitcast(FP8X4),
-                    lhsT_scale=wd_scales[:, n * P : (n + 1) * P],
+                    out=tile[:, at : at + j1 - j0],
+                    lhsT=wd_mx[n][0].bitcast(FP8X4),
+                    lhsT_scale=wd_mx[n][1],
                     rhs=h_codes[:, j0:j1].bitcast(FP8X4),
                     rhs_scale=h_scales[:, j0:j1],
                     start=True,
                     stop=True,
                 )
-            for span in [slice(0, spans[-1].stop)] if one_copy else spans:
-                nc.scalar.copy(y_sb[:, span], y_ps[:, span])
+                at = at + j1 - j0
 
-        def scatter(n, j0, j1):
-            nc.vector.tensor_tensor(windows[n][:].indirect(offsets(dst_list, j0, j1)), y[n, j0], wgo_sb[:, j0:j1], MULT)
+        def evacuate(y_sb, n, j0, width):
+            tile, at = y_ps[n, j0]
+            nc.scalar.copy(y_sb, tile[:, at : at + width])
+
+        def y_tile(name, width, tag=""):
+            return keep.tile([P, width], F32, name=name, tag=tag)
+
+        def scatter(n, j0, j1, y_sb):
+            nc.vector.tensor_tensor(windows[n][:].indirect(offsets(dst_list, j0, j1)), y_sb, wgo_sb[:, j0:j1], MULT)
 
         def store(n):
             nc.sync.dma_start(out[n * P : (n + 1) * P, :], windows[n][:])
@@ -178,59 +223,84 @@ def tile_list_msg_silu_none_kernel(
         gather_scales(0, q0, q1)
         gather_scales(1, q0, q1)
         gather_scales(0, q1, q2)
-        gather_scales(1, q1, q2)
-        gather_scales(0, q2, q3)
-        gather_words(0, q0, q1)
+        gather_words(0, q0, q1, AT_FIRST_WORDS)
         gather_words(1, q0, q1)
         gather_words(0, q1, q2)
         gather_words(1, q1, q2)
-        gather_scales(0, q3, q4)
-        gather_scales(1, q2, q4)
         gather_words(0, q2, q4)
-        cast_wd(0, "wd_bf0")
         gather_words(1, q2, q4)
-        quantise_wd(0)
 
-        hidden(0)
+        for half in range(2):
+            for s in range(2):
+                project(0, half, s)
+        gather_scales(1, q1, q4, AT_FIRST_WORDS)
+        cast_wd(nc.vector.tensor_copy, 0, 1)
+        activate(0, 0)
+        activate(0, 1)
+        smooth(0, 0)
+        smooth(0, 1)
+        interleave(0)
         quantise_hidden(0)
-        message([(0, q0, q1), (1, q0, q1)], "y_ps", 2, "y01_0", one_copy=False)
-        cast_wd(1, "grouped0")
-        quantise_wd(1)
-        scatter(0, q0, q1)
-        scatter(1, q0, q1)
-
-        hidden(1)
-        quantise_hidden(1)
-        windows[3] = keep.tile([P, T], F32, name="window3", tag="grouped1", align_bytes=64)
+        quantise_wd(0, 1, AT_PLANES0)
+        gather_scales(0, q2, q4, AT_PLANES0 + 512)
+        cast_wd(nc.scalar.copy, 1, 3, AT_PLANES0 + 1024)
+        quantise_wd(1, 3)
+        windows[3] = placed([P, T], F32, "window3", AT_PLANES0 + 2048)
         nc.gpsimd.memset(windows[3][:], 0.0)
-        message([(2, q0, q1)], "y2_ps", 1, "planes1")
-        message([(0, q1, q2), (1, q1, q2)], "y_ps", 2, "y01_1")
-        scatter(2, q0, q1)
-        scatter(0, q1, q2)
-        scatter(1, q1, q2)
 
-        hidden(2)
-        quantise_hidden(2)
-        message([(2, q1, q2)], "y2_ps", 1, "planes2")
-        message([(0, q2, q3), (1, q2, q3)], "y_ps", 2, "y01_2")
-        scatter(2, q1, q2)
-        scatter(0, q2, q3)
-        scatter(1, q2, q3)
+        message([(0, q0, q1)], "y0")
+        y_00 = y_tile("y_00", QUARTER)
+        evacuate(y_00[:], 0, q0, QUARTER)
+        scatter(0, q0, q1, y_00[:])
+        message([(1, q0, q1), (2, q0, q1)], "y1")
+        for half in range(2):
+            for s in range(2):
+                project(1, half, s)
+        activate(1, 0)
+        activate(1, 1)
+        y_10 = y_tile("y_10", QUARTER)
+        evacuate(y_10[:], 1, q0, QUARTER)
+        scatter(1, q0, q1, y_10[:])
+        cast_wd(nc.scalar.copy, 3, 4)
+        quantise_wd(3, 4)
+        y_20 = placed([P, QUARTER], F32, "y_20", AT_WD_RAW)
+        evacuate(y_20[:], 2, q0, QUARTER)
+        scatter(2, q0, q1, y_20[:])
+        held = (3, q0, q1)
 
-        hidden(3)
-        quantise_hidden(3)
-        message([(2, q2, q3), (3, q0, q1)], "y2_ps", 1, "planes3")
-        message([(0, q3, q4), (1, q3, q4)], "y_ps", 2, "y01_3")
-        message([(2, q3, q4), (3, q3, q4)], "y_ps", 2, "y23_3")
-        message([(3, q1, q3)], "y3_ps", 1, "y01_3")
-        scatter(2, q2, q3)
-        scatter(3, q0, q1)
-        scatter(0, q3, q4)
+        for q in range(1, 4):
+            j0, j1 = q * QUARTER, (q + 1) * QUARTER
+            if q > 1:
+                for half in range(2):
+                    for s in range(2):
+                        project(q, half, s)
+                activate(q, 0)
+                activate(q, 1)
+            message([held], "y2")
+            smooth(q, 0)
+            smooth(q, 1)
+            interleave(q)
+            quantise_hidden(q)
+            y_held = y_tile("y_held%d" % q, QUARTER, "planes%d" % q)
+            evacuate(y_held[:], held[0], held[1], QUARTER)
+            scatter(held[0], held[1], held[2], y_held[:])
+            message([(0, j0, j1), (1, j0, j1)], "y%d" % (1 - q % 2))
+            y_01 = y_tile("y_01_%d" % q, 2 * QUARTER)
+            evacuate(y_01[:], 0, j0, 2 * QUARTER)
+            for n in range(2):
+                scatter(n, j0, j1, y_01[:, n * QUARTER : (n + 1) * QUARTER])
+            held = (2, j0, j1)
+
         store(0)
-        scatter(1, q3, q4)
         store(1)
-        scatter(2, q3, q4)
+        message([(2, q3, q4), (3, q3, q4)], "y1")
+        message([(3, q1, q3)], "y3")
+        y_23 = y_tile("y_23", QUARTER)
+        evacuate(y_23[:], 2, q3, QUARTER)
+        scatter(2, q3, q4, y_23[:])
         store(2)
-        scatter(3, q3, q4)
-        scatter(3, q1, q3)
+        y_last = keep.tile([P, 3 * QUARTER], F32, name="y_last", tag="grouped3", align_bytes=64)
+        evacuate(y_last[:, 0 : 2 * QUARTER], 3, q1, 2 * QUARTER)
+        evacuate(y_last[:, 2 * QUARTER :], 3, q3, QUARTER)
+        scatter(3, q1, q4, y_last[:])
         store(3)

@@ -19,7 +19,7 @@ MULT = mybir.AluOpType.mult
 P = 128
 PACK = 4
 QUARTER = J // 4
-AT_PLANES0 = 0
+AT_PLANES0 = 8704
 AT_WD_RAW = 10240
 AT_FIRST_WORDS = 18432
 
@@ -69,14 +69,13 @@ def tile_list_msg_silu_none_kernel(
         nc.sync.dma_start(tab[:], words(tab_words))
         for r in range(1, 4):
             nc.sync.dma_start(w_planes[0][r:P:32, :], scale_rows(ws_scales, r))
-        nc.sync.dma_start(w_words[0][:], words(ws_words))
         for r in range(4):
-            queue = nc.sync if r < 2 else nc.gpsimd
-            queue.dma_start(w_planes[1][r:P:32, :], scale_rows(wt_scales, r))
-        nc.sync.dma_start(w_words[1][:], words(wt_words))
-        nc.sync.dma_start(sm_sb[:], sm.rearrange("(p t) -> p t", t=PACK))
+            nc.sync.dma_start(w_planes[1][r:P:32, :], scale_rows(wt_scales, r))
         nc.sync.dma_start(wd_raw[:], wd.rearrange("(p t) n -> p t n", t=PACK))
         nc.sync.dma_start(wgo_sb[:], wgo)
+        nc.gpsimd.dma_start(sm_sb[:], sm.rearrange("(p t) -> p t", t=PACK))
+        nc.gpsimd.dma_start(w_words[0][:], words(ws_words))
+        nc.gpsimd.dma_start(w_words[1][:], words(wt_words))
 
         windows = {}
         for n in range(3):
@@ -148,7 +147,7 @@ def tile_list_msg_silu_none_kernel(
         def smooth(q, half):
             j = q * QUARTER + half * P
             if half == 0 and q == 0:
-                h_planes[q] = placed([P, PACK, QUARTER], BF16, "h_planes0", AT_PLANES0)
+                h_planes[q] = placed([P, PACK, P], BF16, "h_planes0", AT_PLANES0)
             elif half == 0:
                 h_planes[q] = keep.tile([P, PACK, QUARTER], BF16, name="h_planes", tag="planes%d" % q)
             for t in range(PACK):
@@ -223,29 +222,39 @@ def tile_list_msg_silu_none_kernel(
         gather_scales(0, q0, q1)
         gather_scales(1, q0, q1)
         gather_scales(0, q1, q2)
+        gather_scales(1, q1, q2)
         gather_words(0, q0, q1, AT_FIRST_WORDS)
         gather_words(1, q0, q1)
         gather_words(0, q1, q2)
         gather_words(1, q1, q2)
         gather_words(0, q2, q4)
-        gather_words(1, q2, q4)
 
         for half in range(2):
             for s in range(2):
                 project(0, half, s)
-        gather_scales(1, q1, q4, AT_FIRST_WORDS)
+        gather_scales(1, q2, q4, AT_FIRST_WORDS)
+        gather_words(1, q2, q4, AT_FIRST_WORDS + 512)
         cast_wd(nc.vector.tensor_copy, 0, 1)
         activate(0, 0)
         activate(0, 1)
         smooth(0, 0)
-        smooth(0, 1)
-        interleave(0)
+        h_grouped[0] = keep.tile([P, QUARTER, PACK], BF16, name="h_grouped0", align_bytes=64)
+        nc.vector.tensor_tensor(
+            h_grouped[0][:, P:QUARTER, :],
+            act_t[P][:].rearrange("p t j -> p j t"),
+            sm_sb[:].unsqueeze(1).to_broadcast([P, P, PACK]),
+            MULT,
+        )
+        nc.scalar.copy(
+            h_grouped[0][:, 0:P, :].rearrange("p (c i) t -> p c t i", i=4),
+            h_planes[0][:].rearrange("p t (c i) -> p c t i", i=4),
+        )
+        quantise_wd(0, 1, AT_PLANES0 + 448)
         quantise_hidden(0)
-        quantise_wd(0, 1, AT_PLANES0)
-        gather_scales(0, q2, q4, AT_PLANES0 + 512)
-        cast_wd(nc.scalar.copy, 1, 3, AT_PLANES0 + 1024)
+        gather_scales(0, q2, q4, AT_PLANES0 + 960)
+        cast_wd(nc.scalar.copy, 1, 3, AT_PLANES0 - 1600)
         quantise_wd(1, 3)
-        windows[3] = placed([P, T], F32, "window3", AT_PLANES0 + 2048)
+        windows[3] = placed([P, T], F32, "window3", 0)
         nc.gpsimd.memset(windows[3][:], 0.0)
 
         message([(0, q0, q1)], "y0")
@@ -266,41 +275,41 @@ def tile_list_msg_silu_none_kernel(
         y_20 = placed([P, QUARTER], F32, "y_20", AT_WD_RAW)
         evacuate(y_20[:], 2, q0, QUARTER)
         scatter(2, q0, q1, y_20[:])
-        held = (3, q0, q1)
 
-        for q in range(1, 4):
-            j0, j1 = q * QUARTER, (q + 1) * QUARTER
-            if q > 1:
-                for half in range(2):
-                    for s in range(2):
-                        project(q, half, s)
-                activate(q, 0)
-                activate(q, 1)
-            message([held], "y2")
+        def piece(n, j0, j1, bank, tag=""):
+            message([(n, j0, j1)], bank)
+            y_sb = y_tile("y_%d_%d" % (n, j0), j1 - j0, tag)
+            evacuate(y_sb[:], n, j0, j1 - j0)
+            scatter(n, j0, j1, y_sb[:])
+
+        def finish_hidden(q):
             smooth(q, 0)
             smooth(q, 1)
             interleave(q)
             quantise_hidden(q)
-            y_held = y_tile("y_held%d" % q, QUARTER, "planes%d" % q)
-            evacuate(y_held[:], held[0], held[1], QUARTER)
-            scatter(held[0], held[1], held[2], y_held[:])
-            message([(0, j0, j1), (1, j0, j1)], "y%d" % (1 - q % 2))
-            y_01 = y_tile("y_01_%d" % q, 2 * QUARTER)
-            evacuate(y_01[:], 0, j0, 2 * QUARTER)
-            for n in range(2):
-                scatter(n, j0, j1, y_01[:, n * QUARTER : (n + 1) * QUARTER])
-            held = (2, j0, j1)
 
-        store(0)
-        store(1)
-        message([(2, q3, q4), (3, q3, q4)], "y1")
-        message([(3, q1, q3)], "y3")
-        y_23 = y_tile("y_23", QUARTER)
-        evacuate(y_23[:], 2, q3, QUARTER)
-        scatter(2, q3, q4, y_23[:])
-        store(2)
-        y_last = keep.tile([P, 3 * QUARTER], F32, name="y_last", tag="grouped3", align_bytes=64)
-        evacuate(y_last[:, 0 : 2 * QUARTER], 3, q1, 2 * QUARTER)
-        evacuate(y_last[:, 2 * QUARTER :], 3, q3, QUARTER)
-        scatter(3, q1, q4, y_last[:])
+        def start_hidden(q):
+            for half in range(2):
+                for s in range(2):
+                    project(q, half, s)
+            activate(q, 0)
+            activate(q, 1)
+
+        finish_hidden(1)
+        piece(3, q0, q1, "y2", "planes1")
+        start_hidden(2)
+        piece(0, q1, q2, "y0")
+        piece(1, q1, q2, "y1")
+        piece(2, q1, q2, "y3")
+        finish_hidden(2)
+        piece(3, q1, q2, "y2", "planes2")
+        start_hidden(3)
+        piece(0, q2, q3, "y0")
+        piece(1, q2, q3, "y1")
+        finish_hidden(3)
+        piece(2, q2, q3, "y3", "planes3")
+        for n in range(3):
+            piece(n, q3, q4, "y%d" % n)
+            store(n)
+        piece(3, q2, q4, "y3")
         store(3)

@@ -46,10 +46,8 @@ def tile_list_msg_silu_none_kernel(
         w_planes = [keep.tile([P, R // 4], I32, name="w_plane%d" % s, align_bytes=64) for s in range(2)]
         ident = keep.tile([P, P], F32, name="ident")
         nc.vector.memset(tab_plane[:], 0)
-        nc.gpsimd.memset(w_planes[0][:], 0)
-        nc.gpsimd.memset(ident[:], 0.0)
-        nc.gpsimd.memset(w_planes[1][:], 0)
-        make_identity(nc, ident[:], nomemset=True)
+        for s in range(2):
+            nc.vector.memset(w_planes[s][:], 0)
 
         def scale_rows(scales, r):
             return scales[0].rearrange("(q r) t -> r q t", r=4)[r].bitcast(I32)
@@ -60,22 +58,23 @@ def tile_list_msg_silu_none_kernel(
         tab = keep.tile([P, T], I32, name="tab", align_bytes=64)
         w_words = [keep.tile([P, R], I32, name="w_words%d" % s, align_bytes=64) for s in range(2)]
         wd_raw = placed([P, PACK, N], F32, "wd_raw", AT_WD_RAW)
-        wgo_sb = keep.tile([P, J], F32, name="wgo_sb")
+        wgo_first = keep.tile([P, QUARTER], F32, name="wgo_first")
+        wgo_rest = keep.tile([P, J - QUARTER], F32, name="wgo_rest")
         sm_sb = keep.tile([P, PACK], F32, name="sm_sb")
         for r in range(4):
             queue = nc.sync if r < 2 else nc.scalar
             queue.dma_start(tab_plane[r:P:32, :], scale_rows(tab_scales, r))
-        nc.sync.dma_start(w_planes[0][0:P:32, :], scale_rows(ws_scales, 0))
-        nc.sync.dma_start(tab[:], words(tab_words))
-        for r in range(1, 4):
-            nc.sync.dma_start(w_planes[0][r:P:32, :], scale_rows(ws_scales, r))
-        for r in range(4):
-            nc.sync.dma_start(w_planes[1][r:P:32, :], scale_rows(wt_scales, r))
+        for s, scales in enumerate((ws_scales, wt_scales)):
+            for r in range(4):
+                nc.sync.dma_start(w_planes[s][r:P:32, :], scale_rows(scales, r))
+        nc.sync.dma_start(sm_sb[:], sm.rearrange("(p t) -> p t", t=PACK))
+        nc.sync.dma_start(wgo_first[:], wgo[:, 0:QUARTER])
         nc.sync.dma_start(wd_raw[:], wd.rearrange("(p t) n -> p t n", t=PACK))
-        nc.sync.dma_start(wgo_sb[:], wgo)
-        nc.gpsimd.dma_start(sm_sb[:], sm.rearrange("(p t) -> p t", t=PACK))
+        nc.sync.dma_start(wgo_rest[:], wgo[:, QUARTER:J])
+        nc.gpsimd.dma_start(tab[:], words(tab_words))
         nc.gpsimd.dma_start(w_words[0][:], words(ws_words))
         nc.gpsimd.dma_start(w_words[1][:], words(wt_words))
+        make_identity(nc, ident[:])
 
         windows = {}
         for n in range(3):
@@ -213,7 +212,8 @@ def tile_list_msg_silu_none_kernel(
             return keep.tile([P, width], F32, name=name, tag=tag)
 
         def scatter(n, j0, j1, y_sb):
-            nc.vector.tensor_tensor(windows[n][:].indirect(offsets(dst_list, j0, j1)), y_sb, wgo_sb[:, j0:j1], MULT)
+            weights = wgo_first[:] if j0 == 0 else wgo_rest[:, j0 - QUARTER : j1 - QUARTER]
+            nc.vector.tensor_tensor(windows[n][:].indirect(offsets(dst_list, j0, j1)), y_sb, weights, MULT)
 
         def store(n):
             nc.sync.dma_start(out[n * P : (n + 1) * P, :], windows[n][:])

@@ -22,6 +22,7 @@ QUARTER = J // 4
 AT_PLANES0 = 8704
 AT_WD_RAW = 10240
 AT_FIRST_WORDS = 18432
+AT_GROUPED0 = 21504
 
 
 def tile_list_msg_silu_none_kernel(
@@ -46,8 +47,10 @@ def tile_list_msg_silu_none_kernel(
         w_planes = [keep.tile([P, R // 4], I32, name="w_plane%d" % s, align_bytes=64) for s in range(2)]
         ident = keep.tile([P, P], F32, name="ident")
         nc.vector.memset(tab_plane[:], 0)
-        for s in range(2):
-            nc.vector.memset(w_planes[s][:], 0)
+        nc.gpsimd.memset(w_planes[0][:], 0)
+        nc.gpsimd.memset(ident[:], 0.0)
+        nc.gpsimd.memset(w_planes[1][:], 0)
+        make_identity(nc, ident[:], nomemset=True)
 
         def scale_rows(scales, r):
             return scales[0].rearrange("(q r) t -> r q t", r=4)[r].bitcast(I32)
@@ -58,27 +61,29 @@ def tile_list_msg_silu_none_kernel(
         tab = keep.tile([P, T], I32, name="tab", align_bytes=64)
         w_words = [keep.tile([P, R], I32, name="w_words%d" % s, align_bytes=64) for s in range(2)]
         wd_raw = placed([P, PACK, N], F32, "wd_raw", AT_WD_RAW)
-        wgo_first = keep.tile([P, QUARTER], F32, name="wgo_first")
-        wgo_rest = keep.tile([P, J - QUARTER], F32, name="wgo_rest")
+        wgo_sb = keep.tile([P, J], F32, name="wgo_sb")
         sm_sb = keep.tile([P, PACK], F32, name="sm_sb")
         for r in range(4):
             queue = nc.sync if r < 2 else nc.scalar
             queue.dma_start(tab_plane[r:P:32, :], scale_rows(tab_scales, r))
-        for s, scales in enumerate((ws_scales, wt_scales)):
-            for r in range(4):
-                nc.sync.dma_start(w_planes[s][r:P:32, :], scale_rows(scales, r))
+        nc.sync.dma_start(w_planes[0][0:P:32, :], scale_rows(ws_scales, 0))
+        nc.sync.dma_start(tab[:], words(tab_words))
+        for r in range(1, 4):
+            nc.sync.dma_start(w_planes[0][r:P:32, :], scale_rows(ws_scales, r))
+        for r in range(4):
+            nc.sync.dma_start(w_planes[1][r:P:32, :], scale_rows(wt_scales, r))
         nc.sync.dma_start(sm_sb[:], sm.rearrange("(p t) -> p t", t=PACK))
-        nc.sync.dma_start(wgo_first[:], wgo[:, 0:QUARTER])
         nc.sync.dma_start(wd_raw[:], wd.rearrange("(p t) n -> p t n", t=PACK))
-        nc.sync.dma_start(wgo_rest[:], wgo[:, QUARTER:J])
-        nc.gpsimd.dma_start(tab[:], words(tab_words))
-        nc.gpsimd.dma_start(w_words[0][:], words(ws_words))
-        nc.gpsimd.dma_start(w_words[1][:], words(wt_words))
-        make_identity(nc, ident[:])
+        nc.sync.dma_start(wgo_sb[:], wgo)
 
         windows = {}
         for n in range(3):
             windows[n] = keep.tile([P, T], F32, name="window%d" % n)
+        nc.gpsimd.memset(windows[0][:, 0 : T // 2], 0.0)
+        nc.gpsimd.dma_start(w_words[0][:], words(ws_words))
+        nc.gpsimd.dma_start(w_words[1][:], words(wt_words))
+        nc.gpsimd.memset(windows[0][:, T // 2 : T], 0.0)
+        for n in range(1, 3):
             nc.gpsimd.memset(windows[n][:], 0.0)
 
         lists = (src_list, dst_list)
@@ -212,22 +217,18 @@ def tile_list_msg_silu_none_kernel(
             return keep.tile([P, width], F32, name=name, tag=tag)
 
         def scatter(n, j0, j1, y_sb):
-            weights = wgo_first[:] if j0 == 0 else wgo_rest[:, j0 - QUARTER : j1 - QUARTER]
-            nc.vector.tensor_tensor(windows[n][:].indirect(offsets(dst_list, j0, j1)), y_sb, weights, MULT)
+            nc.vector.tensor_tensor(windows[n][:].indirect(offsets(dst_list, j0, j1)), y_sb, wgo_sb[:, j0:j1], MULT)
 
         def store(n):
             nc.sync.dma_start(out[n * P : (n + 1) * P, :], windows[n][:])
 
         q0, q1, q2, q3, q4 = range(0, J + 1, QUARTER)
-        gather_scales(0, q0, q1)
-        gather_scales(1, q0, q1)
-        gather_scales(0, q1, q2)
-        gather_scales(1, q1, q2)
+        gather_scales(0, q0, q2)
+        gather_scales(1, q0, q2)
         gather_words(0, q0, q1, AT_FIRST_WORDS)
         gather_words(1, q0, q1)
-        gather_words(0, q1, q2)
         gather_words(1, q1, q2)
-        gather_words(0, q2, q4)
+        gather_words(0, q1, q4)
 
         for half in range(2):
             for s in range(2):
@@ -238,7 +239,7 @@ def tile_list_msg_silu_none_kernel(
         activate(0, 0)
         activate(0, 1)
         smooth(0, 0)
-        h_grouped[0] = keep.tile([P, QUARTER, PACK], BF16, name="h_grouped0", align_bytes=64)
+        h_grouped[0] = placed([P, QUARTER, PACK], BF16, "h_grouped0", AT_GROUPED0)
         nc.vector.tensor_tensor(
             h_grouped[0][:, P:QUARTER, :],
             act_t[P][:].rearrange("p t j -> p j t"),
@@ -258,19 +259,19 @@ def tile_list_msg_silu_none_kernel(
         nc.gpsimd.memset(windows[3][:], 0.0)
 
         message([(0, q0, q1)], "y0")
-        y_00 = y_tile("y_00", QUARTER)
-        evacuate(y_00[:], 0, q0, QUARTER)
-        scatter(0, q0, q1, y_00[:])
         message([(1, q0, q1), (2, q0, q1)], "y1")
         for half in range(2):
             for s in range(2):
                 project(1, half, s)
         activate(1, 0)
+        y_00 = y_tile("y_00", QUARTER)
+        evacuate(y_00[:], 0, q0, QUARTER)
+        scatter(0, q0, q1, y_00[:])
         activate(1, 1)
         y_10 = y_tile("y_10", QUARTER)
         evacuate(y_10[:], 1, q0, QUARTER)
         scatter(1, q0, q1, y_10[:])
-        cast_wd(nc.scalar.copy, 3, 4)
+        cast_wd(nc.scalar.copy, 3, 4, AT_GROUPED0)
         quantise_wd(3, 4)
         y_20 = placed([P, QUARTER], F32, "y_20", AT_WD_RAW)
         evacuate(y_20[:], 2, q0, QUARTER)
@@ -304,10 +305,10 @@ def tile_list_msg_silu_none_kernel(
         finish_hidden(2)
         piece(3, q1, q2, "y2", "planes2")
         start_hidden(3)
-        piece(0, q2, q3, "y0")
-        piece(1, q2, q3, "y1")
+        piece(0, q2, q3, "bank2")
+        piece(1, q2, q3, "bank3")
         finish_hidden(3)
-        piece(2, q2, q3, "y3", "planes3")
+        piece(2, q2, q3, "bank2", "planes3")
         for n in range(3):
             piece(n, q3, q4, "y%d" % n)
             store(n)

@@ -19,10 +19,19 @@ MULT = mybir.AluOpType.mult
 P = 128
 PACK = 4
 QUARTER = J // 4
-AT_PLANES0 = 8704
-AT_WD_RAW = 10240
-AT_FIRST_WORDS = 18432
-AT_GROUPED0 = 21504
+BANK = 512
+SRC, DST = 0, 1
+
+AT_FIRST_SRC_WORDS = 0
+AT_LAST_DST_SCALES = AT_FIRST_SRC_WORDS
+AT_LAST_DST_WORDS = AT_FIRST_SRC_WORDS + 512
+AT_FIRST_DST_WORDS = 4096
+AT_WD_GROUPED = AT_FIRST_DST_WORDS
+AT_LAST_WINDOW = AT_WD_GROUPED
+AT_SECOND_SILU = 16384
+AT_WD_SCALES_FIRST = AT_SECOND_SILU
+AT_FIRST_HIDDEN = 18432
+AT_LAST_SRC_SCALES = AT_FIRST_HIDDEN
 
 
 def tile_list_msg_silu_none_kernel(
@@ -31,284 +40,252 @@ def tile_list_msg_silu_none_kernel(
     nc = tc.nc
     with ExitStack() as ctx:
         keep = ctx.enter_context(tc.tile_pool(name="keep", bufs=1))
-        reuse = ctx.enter_context(tc.tile_pool(name="reuse", bufs=1))
-        ring = ctx.enter_context(tc.tile_pool(name="ring", bufs=2))
+        shared = ctx.enter_context(tc.tile_pool(name="shared", bufs=1))
         psum = ctx.enter_context(tc.psum_pool(name="psum", bufs=1))
 
-        def placed(shape, dtype, name, offset):
-            return reuse.tile(shape, dtype, name=name, offset=offset, align_bytes=64)
+        def sbuf(shape, dtype, name, at=None, tag=""):
+            if at is None:
+                return keep.tile(shape, dtype, name=name, tag=tag, align_bytes=64)
+            return shared.tile(shape, dtype, name=name, offset=at, align_bytes=64)
 
-        src_list = keep.tile([P, J // 16], U16, name="src_list")
-        dst_list = keep.tile([P, J // 16], U16, name="dst_list")
-        nc.sync.dma_start(src_list[:], offs)
-        nc.sync.dma_start(dst_list[:], offs2)
+        lists = [keep.tile([P, J // 16], U16, name="list%d" % s) for s in (SRC, DST)]
+        nc.sync.dma_start(lists[SRC][:], offs)
+        nc.sync.dma_start(lists[DST][:], offs2)
 
-        tab_plane = keep.tile([P, T // 4], I32, name="tab_plane", align_bytes=64)
-        w_planes = [keep.tile([P, R // 4], I32, name="w_plane%d" % s, align_bytes=64) for s in range(2)]
-        ident = keep.tile([P, P], F32, name="ident")
+        tab_plane = sbuf([P, T // 4], I32, "tab_plane")
+        w_planes = [sbuf([P, R // 4], I32, "w_plane%d" % s) for s in (SRC, DST)]
+        ident = sbuf([P, P], F32, "ident")
         nc.vector.memset(tab_plane[:], 0)
-        nc.gpsimd.memset(w_planes[0][:], 0)
+        nc.gpsimd.memset(w_planes[SRC][:], 0)
         nc.gpsimd.memset(ident[:], 0.0)
-        nc.gpsimd.memset(w_planes[1][:], 0)
+        nc.gpsimd.memset(w_planes[DST][:], 0)
         make_identity(nc, ident[:], nomemset=True)
 
-        def scale_rows(scales, r):
-            return scales[0].rearrange("(q r) t -> r q t", r=4)[r].bitcast(I32)
+        def load_scale_rows(queue, plane, scales, row):
+            queue.dma_start(plane[row:P:32, :], scales[0].rearrange("(q r) c -> r q c", r=4)[row].bitcast(I32))
 
         def words(packed):
             return packed[0].rearrange("p c i -> p (c i)").bitcast(I32)
 
-        tab = keep.tile([P, T], I32, name="tab", align_bytes=64)
-        w_words = [keep.tile([P, R], I32, name="w_words%d" % s, align_bytes=64) for s in range(2)]
-        wd_raw = placed([P, PACK, N], F32, "wd_raw", AT_WD_RAW)
-        wgo_sb = keep.tile([P, J], F32, name="wgo_sb")
-        sm_sb = keep.tile([P, PACK], F32, name="sm_sb")
-        for r in range(4):
-            queue = nc.sync if r < 2 else nc.scalar
-            queue.dma_start(tab_plane[r:P:32, :], scale_rows(tab_scales, r))
-        nc.sync.dma_start(w_planes[0][0:P:32, :], scale_rows(ws_scales, 0))
+        tab = sbuf([P, T], I32, "tab")
+        w_words = [sbuf([P, R], I32, "w_words%d" % s) for s in (SRC, DST)]
+        wd_raw = sbuf([P, PACK, N], F32, "wd_raw")
+        wgo_sb = sbuf([P, J], F32, "wgo_sb")
+        sm_sb = sbuf([P, PACK], F32, "sm_sb")
+
+        for row in range(4):
+            load_scale_rows(nc.sync if row < 2 else nc.scalar, tab_plane, tab_scales, row)
+        load_scale_rows(nc.sync, w_planes[SRC], ws_scales, 0)
         nc.sync.dma_start(tab[:], words(tab_words))
-        for r in range(1, 4):
-            nc.sync.dma_start(w_planes[0][r:P:32, :], scale_rows(ws_scales, r))
-        for r in range(4):
-            nc.sync.dma_start(w_planes[1][r:P:32, :], scale_rows(wt_scales, r))
-        nc.sync.dma_start(sm_sb[:], sm.rearrange("(p t) -> p t", t=PACK))
-        nc.sync.dma_start(wd_raw[:], wd.rearrange("(p t) n -> p t n", t=PACK))
+        for row in range(1, 4):
+            load_scale_rows(nc.sync, w_planes[SRC], ws_scales, row)
+        for row in range(4):
+            load_scale_rows(nc.sync, w_planes[DST], wt_scales, row)
+        nc.sync.dma_start(sm_sb[:], sm.rearrange("(p i) -> p i", i=PACK))
+        nc.sync.dma_start(wd_raw[:], wd.rearrange("(p i) n -> p i n", i=PACK))
         nc.sync.dma_start(wgo_sb[:], wgo)
 
-        windows = {}
-        for n in range(3):
-            windows[n] = keep.tile([P, T], F32, name="window%d" % n)
+        windows = [sbuf([P, T], F32, "window%d" % n) for n in range(3)]
         nc.gpsimd.memset(windows[0][:, 0 : T // 2], 0.0)
-        nc.gpsimd.dma_start(w_words[0][:], words(ws_words))
-        nc.gpsimd.dma_start(w_words[1][:], words(wt_words))
+        nc.gpsimd.dma_start(w_words[SRC][:], words(ws_words))
+        nc.gpsimd.dma_start(w_words[DST][:], words(wt_words))
         nc.gpsimd.memset(windows[0][:, T // 2 : T], 0.0)
-        for n in range(1, 3):
-            nc.gpsimd.memset(windows[n][:], 0.0)
+        nc.gpsimd.memset(windows[1][:], 0.0)
+        nc.gpsimd.memset(windows[2][:], 0.0)
 
-        lists = (src_list, dst_list)
         v_words = {}
         v_scales = {}
-        wd_bf = {}
-        wd_mx = {}
-        h_codes = keep.tile([P, J], U32, name="h_codes", align_bytes=64)
-        h_scales = keep.tile([P, J], U8, name="h_scales", align_bytes=64)
+        sums = {}
+        turned = {}
+        h_planes = {}
         h_grouped = {}
-        y = {}
+        wd_mx = {}
+        y_psum = {}
+        h_codes = sbuf([P, J], U32, "h_codes")
+        h_scales = sbuf([P, J], U8, "h_scales")
 
-        def offsets(lst, j0, j1):
-            return lst[:, j0 // 16 : j1 // 16]
+        def offsets(s, j0, j1):
+            return lists[s][:, j0 // 16 : j1 // 16]
 
-        def fresh(shape, dtype, name, offset):
-            if offset is None:
-                return keep.tile(shape, dtype, name=name, align_bytes=64)
-            return placed(shape, dtype, name, offset)
-
-        def gather(picked, window, dtype, name, s, j0, j1, offset):
-            tile = fresh([P, j1 - j0], dtype, "%s%d_%d" % (name, s, j0), offset)
-            nc.vector.tensor_copy(tile[:], window[:].bitcast(dtype).indirect(offsets(lists[s], j0, j1)))
+        def gather(picked, window, dtype, name, s, j0, j1, at):
+            tile = sbuf([P, j1 - j0], dtype, "%s%d_%d" % (name, s, j0), at)
+            nc.vector.tensor_copy(tile[:], window[:].bitcast(dtype).indirect(offsets(s, j0, j1)))
             for j in range(j0, j1, P):
                 picked[s, j] = tile[:, j - j0 : j - j0 + P]
 
-        def gather_scales(s, j0, j1, offset=None):
-            gather(v_scales, tab_plane, U8, "v_scales", s, j0, j1, offset)
+        def gather_scales(s, j0, j1, at=None):
+            gather(v_scales, tab_plane, U8, "v_scales", s, j0, j1, at)
 
-        def gather_words(s, j0, j1, offset=None):
-            gather(v_words, tab, U32, "v_words", s, j0, j1, offset)
+        def gather_words(s, j0, j1, at=None):
+            gather(v_words, tab, U32, "v_words", s, j0, j1, at)
 
-        a_ps = {}
-        act = {}
-        act_t = {}
-        h_planes = {}
+        def bank(q, tile, role):
+            swapped = q % 2 if tile == 0 else max(q - 1, 0) % 2
+            return "pair%d_%d" % (tile, (swapped + role) % 2)
 
-        def project(q, half, s):
-            j = q * QUARTER + half * P
-            if s == 0:
-                a_ps[j] = psum.tile([P, R], F32, name="a_ps", tag="bank%d" % (2 * (q % 2) + half))
-            nc.tensor.matmul_mx(
-                out=a_ps[j][:],
-                lhsT=v_words[s, j].bitcast(FP8X4),
-                lhsT_scale=v_scales[s, j],
-                rhs=w_words[s][:].bitcast(FP8X4),
-                rhs_scale=w_planes[s][:].bitcast(U8),
-                start=(s == 0),
-                stop=(s == 1),
-            )
+        def sum_bank(q, tile):
+            return bank(q, tile, 0)
 
-        def activate(q, half):
-            j = q * QUARTER + half * P
-            act[j] = ring.tile([P, PACK, P], F32, name="act")
-            act_t[j] = psum.tile([P, PACK, P], F32, name="act_t", tag="bank%d" % (2 * (1 - q % 2) + half))
-            step = 2 if j == 0 else PACK
-            for t0 in range(0, PACK, step):
-                planes = slice(t0, t0 + step)
-                nc.scalar.activation(
-                    act[j][:, planes, :], a_ps[j][:].rearrange("j (p t) -> j t p", t=PACK)[:, planes, :], ACT.Silu
-                )
-                for t in range(t0, t0 + step):
-                    nc.tensor.transpose(act_t[j][:, t, :], act[j][:, t, :], ident[:])
-
-        def smooth(q, half):
-            j = q * QUARTER + half * P
-            if half == 0 and q == 0:
-                h_planes[q] = placed([P, PACK, P], BF16, "h_planes0", AT_PLANES0)
-            elif half == 0:
-                h_planes[q] = keep.tile([P, PACK, QUARTER], BF16, name="h_planes", tag="planes%d" % q)
-            for t in range(PACK):
-                nc.scalar.activation(
-                    h_planes[q][:, t, half * P : (half + 1) * P], act_t[j][:, t, :], ACT.Copy, scale=sm_sb[:, t : t + 1]
+        def project(q, tile):
+            j = q * QUARTER + tile * P
+            sums[q, tile] = psum.tile([P, R], F32, name="sums", tag=sum_bank(q, tile))
+            for s in (SRC, DST):
+                nc.tensor.matmul_mx(
+                    out=sums[q, tile][:],
+                    lhsT=v_words[s, j].bitcast(FP8X4),
+                    lhsT_scale=v_scales[s, j],
+                    rhs=w_words[s][:].bitcast(FP8X4),
+                    rhs_scale=w_planes[s][:].bitcast(U8),
+                    start=(s == SRC),
+                    stop=(s == DST),
                 )
 
-        def interleave(q):
-            h_grouped[q] = keep.tile([P, QUARTER, PACK], BF16, name="h_grouped%d" % q, tag="grouped%d" % q, align_bytes=64)
+        def activate(q, tile, parts=1, at=None):
+            act = sbuf([P, PACK, P], F32, "act%d_%d" % (q, tile), at)
+            turned[q, tile] = psum.tile([P, PACK, P], F32, name="turned", tag=bank(q, tile, 1))
+            by_plane = sums[q, tile][:].rearrange("j (p i) -> j i p", i=PACK)
+            step = PACK // parts
+            for i0 in range(0, PACK, step):
+                nc.scalar.activation(act[:, i0 : i0 + step, :], by_plane[:, i0 : i0 + step, :], ACT.Silu)
+                for i in range(i0, i0 + step):
+                    nc.tensor.transpose(turned[q, tile][:, i, :], act[:, i, :], ident[:])
+
+        def interleave(grouped, planes):
             nc.scalar.copy(
-                h_grouped[q][:].rearrange("p (c i) t -> p c t i", i=4),
-                h_planes[q][:].rearrange("p t (c i) -> p c t i", i=4),
+                grouped.rearrange("p (c k) i -> p c i k", k=4), planes.rearrange("p i (c k) -> p c i k", k=4)
             )
+
+        def smooth_on_vector(q, at):
+            h_grouped[q] = sbuf([P, QUARTER, PACK], BF16, "h_grouped%d" % q, at)
+            for tile in range(2):
+                nc.vector.tensor_tensor(
+                    h_grouped[q][:, tile * P : (tile + 1) * P, :],
+                    turned[q, tile][:].rearrange("p i j -> p j i"),
+                    sm_sb[:].unsqueeze(1).to_broadcast([P, P, PACK]),
+                    MULT,
+                )
+
+        def smooth_on_scalar(q, tiles):
+            h_planes[q] = sbuf([P, PACK, QUARTER], BF16, "h_planes", tag="planes%d" % q)
+            for tile in tiles:
+                for i in range(PACK):
+                    nc.scalar.activation(
+                        h_planes[q][:, i, tile * P : (tile + 1) * P],
+                        turned[q, tile][:, i, :],
+                        ACT.Copy,
+                        scale=sm_sb[:, i : i + 1],
+                    )
+            h_grouped[q] = sbuf([P, QUARTER, PACK], BF16, "h_grouped%d" % q)
+            interleave(h_grouped[q][:], h_planes[q][:])
 
         def quantise_hidden(q):
             cols = slice(q * QUARTER, (q + 1) * QUARTER)
             nc.vector.quantize_mx(
                 out=h_codes[:, cols].bitcast(FP8X4),
                 scales=h_scales[:, cols],
-                in_=h_grouped[q][:].rearrange("p j t -> p (j t)"),
+                in_=h_grouped[q][:].rearrange("p j i -> p (j i)"),
             )
 
-        def cast_wd(copy, n0, n1, offset=None):
-            wd_bf[n0] = fresh([P, (n1 - n0) * P, PACK], BF16, "wd_bf%d" % n0, offset)
-            copy(
-                wd_bf[n0][:].rearrange("p (c i) t -> p c t i", i=4),
-                wd_raw[:, :, n0 * P : n1 * P].rearrange("p t (c i) -> p c t i", i=4),
-            )
+        def round_wd(n0, n1):
+            interleave(wd_grouped[:, n0 * P : n1 * P, :], wd_raw[:, :, n0 * P : n1 * P])
 
-        def quantise_wd(n0, n1, offset=None):
-            codes = fresh([P, (n1 - n0) * P], U32, "wd_codes%d" % n0, offset)
-            scales = keep.tile([P, (n1 - n0) * P], U8, name="wd_scales%d" % n0, align_bytes=64)
+        def quantise_wd(n0, n1, at=None):
+            codes = sbuf([P, (n1 - n0) * P], U32, "wd_codes%d" % n0)
+            scales = sbuf([P, (n1 - n0) * P], U8, "wd_scales%d" % n0, at)
             nc.vector.quantize_mx(
-                out=codes[:].bitcast(FP8X4), scales=scales[:], in_=wd_bf[n0][:].rearrange("p n t -> p (n t)")
+                out=codes[:].bitcast(FP8X4),
+                scales=scales[:],
+                in_=wd_grouped[:, n0 * P : n1 * P, :].rearrange("p n i -> p (n i)"),
             )
             for n in range(n0, n1):
                 cols = slice((n - n0) * P, (n - n0 + 1) * P)
                 wd_mx[n] = (codes[:, cols], scales[:, cols])
 
-        y_ps = {}
+        def message(n, j0, j1, y_bank):
+            y_psum[n, j0] = psum.tile([P, BANK], F32, name="y_psum", tag=y_bank)
+            nc.tensor.matmul_mx(
+                out=y_psum[n, j0][:, 0 : j1 - j0],
+                lhsT=wd_mx[n][0].bitcast(FP8X4),
+                lhsT_scale=wd_mx[n][1],
+                rhs=h_codes[:, j0:j1].bitcast(FP8X4),
+                rhs_scale=h_scales[:, j0:j1],
+                start=True,
+                stop=True,
+            )
 
-        def message(pieces, bank):
-            tile = psum.tile([P, 512], F32, name="y_ps", tag=bank)
-            at = 0
-            for n, j0, j1 in pieces:
-                y_ps[n, j0] = (tile, at)
-                nc.tensor.matmul_mx(
-                    out=tile[:, at : at + j1 - j0],
-                    lhsT=wd_mx[n][0].bitcast(FP8X4),
-                    lhsT_scale=wd_mx[n][1],
-                    rhs=h_codes[:, j0:j1].bitcast(FP8X4),
-                    rhs_scale=h_scales[:, j0:j1],
-                    start=True,
-                    stop=True,
-                )
-                at = at + j1 - j0
+        def place(n, j0, j1, tag=""):
+            y = sbuf([P, j1 - j0], F32, "y%d_%d" % (n, j0), tag=tag)
+            nc.scalar.copy(y[:], y_psum[n, j0][:, 0 : j1 - j0])
+            nc.vector.tensor_tensor(windows[n][:].indirect(offsets(DST, j0, j1)), y[:], wgo_sb[:, j0:j1], MULT)
 
-        def evacuate(y_sb, n, j0, width):
-            tile, at = y_ps[n, j0]
-            nc.scalar.copy(y_sb, tile[:, at : at + width])
-
-        def y_tile(name, width, tag=""):
-            return keep.tile([P, width], F32, name=name, tag=tag)
-
-        def scatter(n, j0, j1, y_sb):
-            nc.vector.tensor_tensor(windows[n][:].indirect(offsets(dst_list, j0, j1)), y_sb, wgo_sb[:, j0:j1], MULT)
+        def piece(n, j0, j1, y_bank, tag=""):
+            message(n, j0, j1, y_bank)
+            place(n, j0, j1, tag)
 
         def store(n):
             nc.sync.dma_start(out[n * P : (n + 1) * P, :], windows[n][:])
 
         q0, q1, q2, q3, q4 = range(0, J + 1, QUARTER)
-        gather_scales(0, q0, q2)
-        gather_scales(1, q0, q2)
-        gather_words(0, q0, q1, AT_FIRST_WORDS)
-        gather_words(1, q0, q1)
-        gather_words(1, q1, q2)
-        gather_words(0, q1, q4)
 
-        for half in range(2):
-            for s in range(2):
-                project(0, half, s)
-        gather_scales(1, q2, q4, AT_FIRST_WORDS)
-        gather_words(1, q2, q4, AT_FIRST_WORDS + 512)
-        cast_wd(nc.vector.tensor_copy, 0, 1)
-        activate(0, 0)
-        activate(0, 1)
-        smooth(0, 0)
-        h_grouped[0] = placed([P, QUARTER, PACK], BF16, "h_grouped0", AT_GROUPED0)
-        nc.vector.tensor_tensor(
-            h_grouped[0][:, P:QUARTER, :],
-            act_t[P][:].rearrange("p t j -> p j t"),
-            sm_sb[:].unsqueeze(1).to_broadcast([P, P, PACK]),
-            MULT,
-        )
-        nc.scalar.copy(
-            h_grouped[0][:, 0:P, :].rearrange("p (c i) t -> p c t i", i=4),
-            h_planes[0][:].rearrange("p t (c i) -> p c t i", i=4),
-        )
-        quantise_wd(0, 1, AT_PLANES0 + 448)
+        gather_scales(SRC, q0, q2)
+        gather_scales(DST, q0, q3)
+        gather_words(SRC, q0, q1, AT_FIRST_SRC_WORDS)
+        gather_words(DST, q0, q1, AT_FIRST_DST_WORDS)
+        gather_words(DST, q1, q2)
+        gather_words(SRC, q1, q4)
+        project(0, 0)
+        project(0, 1)
+        gather_scales(DST, q3, q4, AT_LAST_DST_SCALES)
+        gather_words(DST, q2, q4, AT_LAST_DST_WORDS)
+
+        activate(0, 0, parts=2)
+        activate(0, 1, at=AT_SECOND_SILU)
+        wd_grouped = sbuf([P, N, PACK], BF16, "wd_grouped", AT_WD_GROUPED)
+        round_wd(0, 1)
+        round_wd(1, 3)
+        round_wd(3, 4)
+        smooth_on_vector(0, AT_FIRST_HIDDEN)
+        quantise_wd(0, 1, AT_WD_SCALES_FIRST)
         quantise_hidden(0)
-        gather_scales(0, q2, q4, AT_PLANES0 + 960)
-        cast_wd(nc.scalar.copy, 1, 3, AT_PLANES0 - 1600)
         quantise_wd(1, 3)
-        windows[3] = placed([P, T], F32, "window3", 0)
+        gather_scales(SRC, q2, q4, AT_LAST_SRC_SCALES)
+        quantise_wd(3, 4)
+        windows.append(sbuf([P, T], F32, "window3", AT_LAST_WINDOW))
         nc.gpsimd.memset(windows[3][:], 0.0)
 
-        message([(0, q0, q1)], "y0")
-        message([(1, q0, q1), (2, q0, q1)], "y1")
-        for half in range(2):
-            for s in range(2):
-                project(1, half, s)
-        activate(1, 0)
-        y_00 = y_tile("y_00", QUARTER)
-        evacuate(y_00[:], 0, q0, QUARTER)
-        scatter(0, q0, q1, y_00[:])
+        message(0, q0, q1, "y0")
+        project(1, 1)
+        project(1, 0)
         activate(1, 1)
-        y_10 = y_tile("y_10", QUARTER)
-        evacuate(y_10[:], 1, q0, QUARTER)
-        scatter(1, q0, q1, y_10[:])
-        cast_wd(nc.scalar.copy, 3, 4, AT_GROUPED0)
-        quantise_wd(3, 4)
-        y_20 = placed([P, QUARTER], F32, "y_20", AT_WD_RAW)
-        evacuate(y_20[:], 2, q0, QUARTER)
-        scatter(2, q0, q1, y_20[:])
+        activate(1, 0)
+        place(0, q0, q1)
+        piece(1, q0, q1, sum_bank(1, 0))
+        piece(2, q0, q1, "y0")
+        smooth_on_scalar(1, (1, 0))
+        quantise_hidden(1)
+        piece(3, q0, q1, sum_bank(1, 0), "planes1")
 
-        def piece(n, j0, j1, bank, tag=""):
-            message([(n, j0, j1)], bank)
-            y_sb = y_tile("y_%d_%d" % (n, j0), j1 - j0, tag)
-            evacuate(y_sb[:], n, j0, j1 - j0)
-            scatter(n, j0, j1, y_sb[:])
-
-        def finish_hidden(q):
-            smooth(q, 0)
-            smooth(q, 1)
-            interleave(q)
-            quantise_hidden(q)
-
-        def start_hidden(q):
-            for half in range(2):
-                for s in range(2):
-                    project(q, half, s)
-            activate(q, 0)
-            activate(q, 1)
-
-        finish_hidden(1)
-        piece(3, q0, q1, "y2", "planes1")
-        start_hidden(2)
+        project(2, 0)
+        project(2, 1)
+        activate(2, 0)
+        activate(2, 1)
         piece(0, q1, q2, "y0")
         piece(1, q1, q2, "y1")
         piece(2, q1, q2, "y3")
-        finish_hidden(2)
+        smooth_on_scalar(2, (0, 1))
+        quantise_hidden(2)
         piece(3, q1, q2, "y2", "planes2")
-        start_hidden(3)
-        piece(0, q2, q3, "bank2")
-        piece(1, q2, q3, "bank3")
-        finish_hidden(3)
-        piece(2, q2, q3, "bank2", "planes3")
+
+        project(3, 0)
+        project(3, 1)
+        activate(3, 0)
+        activate(3, 1)
+        piece(0, q2, q3, sum_bank(3, 0))
+        piece(1, q2, q3, sum_bank(3, 1))
+        smooth_on_scalar(3, (0, 1))
+        quantise_hidden(3)
+        piece(2, q2, q3, sum_bank(3, 0), "planes3")
+
         for n in range(3):
             piece(n, q3, q4, "y%d" % n)
             store(n)

@@ -50,12 +50,10 @@ def tile_list_msg_silu_none_kernel(
 
         lists = [keep.tile([P, J // 16], U16, name="list%d" % s) for s in (SRC, DST)]
         nc.sync.dma_start(lists[SRC][:], offs)
-        nc.sync.dma_start(lists[DST][:], offs2)
 
         tab_plane = sbuf([P, T // 4], I32, "tab_plane")
         w_planes = [sbuf([P, R // 4], I32, "w_plane%d" % s) for s in (SRC, DST)]
         ident = sbuf([P, P], F32, "ident")
-        nc.vector.memset(tab_plane[:], 0)
         nc.gpsimd.memset(w_planes[SRC][:], 0)
         nc.gpsimd.memset(ident[:], 0.0)
         nc.gpsimd.memset(w_planes[DST][:], 0)
@@ -73,8 +71,11 @@ def tile_list_msg_silu_none_kernel(
         wgo_sb = sbuf([P, J], F32, "wgo_sb")
         sm_sb = sbuf([P, PACK], F32, "sm_sb")
 
-        for row in range(4):
-            load_scale_rows(nc.sync if row < 2 else nc.scalar, tab_plane, tab_scales, row)
+        for quadrant in range(4):
+            rows = tab_scales[0, 4 * quadrant : 4 * quadrant + 4].bitcast(I32)
+            queue = nc.sync if quadrant < 2 else nc.scalar
+            queue.dma_start(tab_plane[32 * quadrant : 32 * quadrant + 32, :], rows.unsqueeze(0).to_broadcast([8, 4, T // 4]))
+        nc.sync.dma_start(lists[DST][:], offs2)
         load_scale_rows(nc.sync, w_planes[SRC], ws_scales, 0)
         nc.sync.dma_start(tab[:], words(tab_words))
         for row in range(1, 4):
@@ -86,10 +87,10 @@ def tile_list_msg_silu_none_kernel(
         nc.sync.dma_start(wgo_sb[:], wgo)
 
         windows = [sbuf([P, T], F32, "window%d" % n) for n in range(3)]
-        nc.gpsimd.memset(windows[0][:, 0 : T // 2], 0.0)
+        nc.gpsimd.memset(windows[0][:, 0 : T // 4], 0.0)
         nc.gpsimd.dma_start(w_words[SRC][:], words(ws_words))
         nc.gpsimd.dma_start(w_words[DST][:], words(wt_words))
-        nc.gpsimd.memset(windows[0][:, T // 2 : T], 0.0)
+        nc.gpsimd.memset(windows[0][:, T // 4 : T], 0.0)
         nc.gpsimd.memset(windows[1][:], 0.0)
         nc.gpsimd.memset(windows[2][:], 0.0)
 

@@ -23,8 +23,7 @@ BANK = 512
 SRC, DST = 0, 1
 
 AT_FIRST_SRC_WORDS = 0
-AT_LAST_DST_SCALES = AT_FIRST_SRC_WORDS
-AT_LAST_DST_WORDS = AT_FIRST_SRC_WORDS + 512
+AT_LAST_DST_WORDS = AT_FIRST_SRC_WORDS
 AT_FIRST_DST_WORDS = 4096
 AT_WD_GROUPED = AT_FIRST_DST_WORDS
 AT_LAST_WINDOW = AT_WD_GROUPED
@@ -229,14 +228,13 @@ def tile_list_msg_silu_none_kernel(
         q0, q1, q2, q3, q4 = range(0, J + 1, QUARTER)
 
         gather_scales(SRC, q0, q2)
-        gather_scales(DST, q0, q3)
+        gather_scales(DST, q0, q4)
         gather_words(SRC, q0, q1, AT_FIRST_SRC_WORDS)
         gather_words(DST, q0, q1, AT_FIRST_DST_WORDS)
         gather_words(DST, q1, q2)
         gather_words(SRC, q1, q4)
         project(0, 0)
         project(0, 1)
-        gather_scales(DST, q3, q4, AT_LAST_DST_SCALES)
         gather_words(DST, q2, q4, AT_LAST_DST_WORDS)
 
         activate(0, 0, parts=2)

@@ -165,16 +165,19 @@ def tile_list_msg_silu_none_kernel(
                     MULT,
                 )
 
+        def scale_planes(q, tile):
+            for i in range(PACK):
+                nc.scalar.activation(
+                    h_planes[q][:, i, tile * P : (tile + 1) * P],
+                    turned[q, tile][:, i, :],
+                    ACT.Copy,
+                    scale=sm_sb[:, i : i + 1],
+                )
+
         def smooth_on_scalar(q, tiles):
             h_planes[q] = sbuf([P, PACK, QUARTER], BF16, "h_planes", tag="planes%d" % q)
             for tile in tiles:
-                for i in range(PACK):
-                    nc.scalar.activation(
-                        h_planes[q][:, i, tile * P : (tile + 1) * P],
-                        turned[q, tile][:, i, :],
-                        ACT.Copy,
-                        scale=sm_sb[:, i : i + 1],
-                    )
+                scale_planes(q, tile)
             h_grouped[q] = sbuf([P, QUARTER, PACK], BF16, "h_grouped%d" % q)
             interleave(h_grouped[q][:], h_planes[q][:])
 
@@ -203,8 +206,11 @@ def tile_list_msg_silu_none_kernel(
 
         def message(n, j0, j1, y_bank):
             y_psum[n, j0] = psum.tile([P, BANK], F32, name="y_psum", tag=y_bank)
+            product(y_psum[n, j0][:, 0 : j1 - j0], n, j0, j1)
+
+        def product(y_out, n, j0, j1):
             nc.tensor.matmul_mx(
-                out=y_psum[n, j0][:, 0 : j1 - j0],
+                out=y_out,
                 lhsT=wd_mx[n][0].bitcast(FP8X4),
                 lhsT_scale=wd_mx[n][1],
                 rhs=h_codes[:, j0:j1].bitcast(FP8X4),
@@ -213,10 +219,13 @@ def tile_list_msg_silu_none_kernel(
                 stop=True,
             )
 
-        def place(n, j0, j1, tag=""):
-            y = sbuf([P, j1 - j0], F32, "y%d_%d" % (n, j0), tag=tag)
+        def scatter(n, j0, j1, y):
+            nc.vector.tensor_tensor(windows[n][:].indirect(offsets(DST, j0, j1)), y, wgo_sb[:, j0:j1], MULT)
+
+        def place(n, j0, j1, tag="", at=None):
+            y = sbuf([P, j1 - j0], F32, "y%d_%d" % (n, j0), at, tag)
             nc.scalar.copy(y[:], y_psum[n, j0][:, 0 : j1 - j0])
-            nc.vector.tensor_tensor(windows[n][:].indirect(offsets(DST, j0, j1)), y[:], wgo_sb[:, j0:j1], MULT)
+            scatter(n, j0, j1, y[:])
 
         def piece(n, j0, j1, y_bank, tag=""):
             message(n, j0, j1, y_bank)
@@ -264,24 +273,38 @@ def tile_list_msg_silu_none_kernel(
         quantise_hidden(1)
         piece(3, q0, q1, sum_bank(1, 0), "planes1")
 
-        project(2, 0)
-        project(2, 1)
-        activate(2, 0)
-        activate(2, 1)
-        piece(0, q1, q2, "y0")
-        piece(1, q1, q2, "y1")
-        piece(2, q1, q2, "y3")
-        smooth_on_scalar(2, (0, 1))
-        quantise_hidden(2)
-        piece(3, q1, q2, "y2", "planes2")
+        def planes_tile(q):
+            h_planes[q] = sbuf([P, PACK, QUARTER], BF16, "h_planes", tag="planes%d" % q)
 
-        project(3, 0)
+        def group(q):
+            h_grouped[q] = sbuf([P, QUARTER, PACK], BF16, "h_grouped%d" % q)
+            interleave(h_grouped[q][:], h_planes[q][:])
+
+        project(2, 1)
+        project(2, 0)
+        activate(2, 1)
+        message(0, q1, q2, sum_bank(2, 1))
+        activate(2, 0)
+        place(0, q1, q2)
+        planes_tile(2)
+        scale_planes(2, 1)
+        piece(1, q1, q2, sum_bank(2, 0))
+        scale_planes(2, 0)
+        piece(2, q1, q2, sum_bank(2, 1))
+        group(2)
+        quantise_hidden(2)
+        piece(3, q1, q2, sum_bank(2, 0), "planes2")
+
         project(3, 1)
-        activate(3, 0)
+        project(3, 0)
         activate(3, 1)
+        activate(3, 0)
+        planes_tile(3)
+        scale_planes(3, 1)
+        scale_planes(3, 0)
         piece(0, q2, q3, sum_bank(3, 0))
-        piece(1, q2, q3, sum_bank(3, 1))
-        smooth_on_scalar(3, (0, 1))
+        piece(1, q2, q3, bank(3, 1, 1))
+        group(3)
         quantise_hidden(3)
         piece(2, q2, q3, sum_bank(3, 0), "planes3")
 

@@ -302,14 +302,16 @@ def tile_list_msg_silu_none_kernel(
         planes_tile(3)
         scale_planes(3, 1)
         scale_planes(3, 0)
+        h_grouped[3] = sbuf([P, QUARTER, PACK], BF16, "h_grouped3")
+        interleave(h_grouped[3][:, P : 2 * P, :], h_planes[3][:, :, P : 2 * P])
         piece(0, q2, q3, sum_bank(3, 0))
-        piece(1, q2, q3, bank(3, 1, 1))
-        group(3)
+        interleave(h_grouped[3][:, 0:P, :], h_planes[3][:, :, 0:P])
         quantise_hidden(3)
-        piece(2, q2, q3, sum_bank(3, 0), "planes3")
+        piece(1, q2, q3, sum_bank(3, 0), "planes3")
 
-        for n in range(3):
+        for n in range(2):
             piece(n, q3, q4, "y%d" % n)
             store(n)
-        piece(3, q2, q4, "y3")
-        store(3)
+        for n in range(2, 4):
+            piece(n, q2, q4, "y%d" % n)
+            store(n)

@@ -22,10 +22,11 @@ QUARTER = J // 4
 BANK = 512
 SRC, DST = 0, 1
 
-AT_FIRST_SRC_WORDS = 0
-AT_LAST_DST_WORDS = AT_FIRST_SRC_WORDS
-AT_FIRST_DST_WORDS = 4096
-AT_WD_GROUPED = AT_FIRST_DST_WORDS
+AT_FIRST_DST_WORDS = 0
+AT_LAST_DST_WORDS = AT_FIRST_DST_WORDS
+AT_FIRST_SRC_WORDS = 3840
+AT_LAST_DST_SCALES = AT_FIRST_SRC_WORDS
+AT_WD_GROUPED = AT_FIRST_SRC_WORDS + 256
 AT_LAST_WINDOW = AT_WD_GROUPED
 AT_SECOND_SILU = 16384
 AT_WD_SCALES_FIRST = AT_SECOND_SILU
@@ -86,10 +87,10 @@ def tile_list_msg_silu_none_kernel(
         nc.sync.dma_start(wgo_sb[:], wgo)
 
         windows = [sbuf([P, T], F32, "window%d" % n) for n in range(3)]
-        nc.gpsimd.memset(windows[0][:, 0 : T // 4], 0.0)
+        nc.gpsimd.memset(windows[0][:, 0 : 3 * T // 8], 0.0)
         nc.gpsimd.dma_start(w_words[SRC][:], words(ws_words))
         nc.gpsimd.dma_start(w_words[DST][:], words(wt_words))
-        nc.gpsimd.memset(windows[0][:, T // 4 : T], 0.0)
+        nc.gpsimd.memset(windows[0][:, 3 * T // 8 : T], 0.0)
         nc.gpsimd.memset(windows[1][:], 0.0)
         nc.gpsimd.memset(windows[2][:], 0.0)
 
@@ -126,18 +127,18 @@ def tile_list_msg_silu_none_kernel(
         def sum_bank(q, tile):
             return bank(q, tile, 0)
 
-        def project(q, tile):
+        def project(q, tile, first=SRC):
             j = q * QUARTER + tile * P
             sums[q, tile] = psum.tile([P, R], F32, name="sums", tag=sum_bank(q, tile))
-            for s in (SRC, DST):
+            for s in (first, 1 - first):
                 nc.tensor.matmul_mx(
                     out=sums[q, tile][:],
                     lhsT=v_words[s, j].bitcast(FP8X4),
                     lhsT_scale=v_scales[s, j],
                     rhs=w_words[s][:].bitcast(FP8X4),
                     rhs_scale=w_planes[s][:].bitcast(U8),
-                    start=(s == SRC),
-                    stop=(s == DST),
+                    start=(s == first),
+                    stop=(s != first),
                 )
 
         def activate(q, tile, parts=1, at=None):
@@ -237,14 +238,15 @@ def tile_list_msg_silu_none_kernel(
         q0, q1, q2, q3, q4 = range(0, J + 1, QUARTER)
 
         gather_scales(SRC, q0, q2)
-        gather_scales(DST, q0, q4)
+        gather_scales(DST, q0, q3)
         gather_words(SRC, q0, q1, AT_FIRST_SRC_WORDS)
         gather_words(DST, q0, q1, AT_FIRST_DST_WORDS)
         gather_words(DST, q1, q2)
         gather_words(SRC, q1, q4)
         project(0, 0)
-        project(0, 1)
+        project(0, 1, first=DST)
         gather_words(DST, q2, q4, AT_LAST_DST_WORDS)
+        gather_scales(DST, q3, q4, AT_LAST_DST_SCALES)
 
         activate(0, 0, parts=2)
         activate(0, 1, at=AT_SECOND_SILU)

@@ -22,8 +22,6 @@ QUARTER = J // 4
 BANK = 512
 SRC, DST = 0, 1
 
-AT_FIRST_DST_WORDS = 0
-AT_LAST_DST_WORDS = AT_FIRST_DST_WORDS
 AT_FIRST_SRC_WORDS = 3840
 AT_LAST_DST_SCALES = AT_FIRST_SRC_WORDS
 AT_WD_GROUPED = AT_FIRST_SRC_WORDS + 256
@@ -31,7 +29,8 @@ AT_LAST_WINDOW = AT_WD_GROUPED
 AT_SECOND_SILU = 16384
 AT_WD_SCALES_FIRST = AT_SECOND_SILU
 AT_FIRST_HIDDEN = 18432
-AT_LAST_SRC_SCALES = AT_FIRST_HIDDEN
+AT_WD_RAW = AT_FIRST_HIDDEN + 2048
+AT_LAST_SRC_SCALES = AT_WD_RAW - 256
 
 
 def tile_list_msg_silu_none_kernel(
@@ -67,7 +66,7 @@ def tile_list_msg_silu_none_kernel(
 
         tab = sbuf([P, T], I32, "tab")
         w_words = [sbuf([P, R], I32, "w_words%d" % s) for s in (SRC, DST)]
-        wd_raw = sbuf([P, PACK, N], F32, "wd_raw")
+        wd_raw = sbuf([P, PACK, N], F32, "wd_raw", AT_WD_RAW)
         wgo_sb = sbuf([P, J], F32, "wgo_sb")
         sm_sb = sbuf([P, PACK], F32, "sm_sb")
 
@@ -240,26 +239,23 @@ def tile_list_msg_silu_none_kernel(
         gather_scales(SRC, q0, q2)
         gather_scales(DST, q0, q3)
         gather_words(SRC, q0, q1, AT_FIRST_SRC_WORDS)
-        gather_words(DST, q0, q1, AT_FIRST_DST_WORDS)
-        gather_words(DST, q1, q2)
+        gather_words(DST, q0, q1)
+        gather_words(DST, q1, q4)
         gather_words(SRC, q1, q4)
         project(0, 0)
         project(0, 1, first=DST)
-        gather_words(DST, q2, q4, AT_LAST_DST_WORDS)
         gather_scales(DST, q3, q4, AT_LAST_DST_SCALES)
 
         activate(0, 0, parts=2)
         activate(0, 1, at=AT_SECOND_SILU)
         wd_grouped = sbuf([P, N, PACK], BF16, "wd_grouped", AT_WD_GROUPED)
-        round_wd(0, 1)
-        round_wd(1, 3)
-        round_wd(3, 4)
+        round_wd(0, 2)
+        round_wd(2, 4)
         smooth_on_vector(0, AT_FIRST_HIDDEN)
-        quantise_wd(0, 1, AT_WD_SCALES_FIRST)
+        quantise_wd(0, 2, AT_WD_SCALES_FIRST)
         quantise_hidden(0)
-        quantise_wd(1, 3)
+        quantise_wd(2, 4)
         gather_scales(SRC, q2, q4, AT_LAST_SRC_SCALES)
-        quantise_wd(3, 4)
         windows.append(sbuf([P, T], F32, "window3", AT_LAST_WINDOW))
         nc.gpsimd.memset(windows[3][:], 0.0)
 

@@ -22,15 +22,14 @@ QUARTER = J // 4
 BANK = 512
 SRC, DST = 0, 1
 
-AT_FIRST_SRC_WORDS = 3840
+AT_FIRST_SRC_WORDS = 0
 AT_LAST_DST_SCALES = AT_FIRST_SRC_WORDS
-AT_WD_GROUPED = AT_FIRST_SRC_WORDS + 256
-AT_LAST_WINDOW = AT_WD_GROUPED
+AT_WD_GROUPED = (2048, 4096)
+AT_FIRST_DST_SCALES = AT_WD_GROUPED[1] - 128
+AT_LAST_DST_WORDS = AT_WD_GROUPED[0]
+AT_LAST_WINDOW = AT_WD_GROUPED[1]
 AT_SECOND_SILU = 16384
 AT_WD_SCALES_FIRST = AT_SECOND_SILU
-AT_FIRST_HIDDEN = 18432
-AT_WD_RAW = AT_FIRST_HIDDEN + 2048
-AT_LAST_SRC_SCALES = AT_WD_RAW - 256
 
 
 def tile_list_msg_silu_none_kernel(
@@ -48,7 +47,7 @@ def tile_list_msg_silu_none_kernel(
             return shared.tile(shape, dtype, name=name, offset=at, align_bytes=64)
 
         lists = [keep.tile([P, J // 16], U16, name="list%d" % s) for s in (SRC, DST)]
-        nc.sync.dma_start(lists[SRC][:], offs)
+        nc.sync.dma_start(lists[DST][:], offs2)
 
         tab_plane = sbuf([P, T // 4], I32, "tab_plane")
         w_planes = [sbuf([P, R // 4], I32, "w_plane%d" % s) for s in (SRC, DST)]
@@ -66,7 +65,7 @@ def tile_list_msg_silu_none_kernel(
 
         tab = sbuf([P, T], I32, "tab")
         w_words = [sbuf([P, R], I32, "w_words%d" % s) for s in (SRC, DST)]
-        wd_raw = sbuf([P, PACK, N], F32, "wd_raw", AT_WD_RAW)
+        wd_raw = [sbuf([P, PACK, N // 2], F32, "wd_raw0"), sbuf([P, PACK, N // 2], F32, "wd_raw1")]
         wgo_sb = sbuf([P, J], F32, "wgo_sb")
         sm_sb = sbuf([P, PACK], F32, "sm_sb")
 
@@ -74,22 +73,24 @@ def tile_list_msg_silu_none_kernel(
             rows = tab_scales[0, 4 * quadrant : 4 * quadrant + 4].bitcast(I32)
             queue = nc.sync if quadrant < 2 else nc.scalar
             queue.dma_start(tab_plane[32 * quadrant : 32 * quadrant + 32, :], rows.unsqueeze(0).to_broadcast([8, 4, T // 4]))
-        nc.sync.dma_start(lists[DST][:], offs2)
-        load_scale_rows(nc.sync, w_planes[SRC], ws_scales, 0)
+        nc.sync.dma_start(lists[SRC][:], offs)
         nc.sync.dma_start(tab[:], words(tab_words))
+        load_scale_rows(nc.sync, w_planes[SRC], ws_scales, 0)
+        nc.sync.dma_start(w_words[SRC][:], words(ws_words))
         for row in range(1, 4):
             load_scale_rows(nc.sync, w_planes[SRC], ws_scales, row)
         for row in range(4):
             load_scale_rows(nc.sync, w_planes[DST], wt_scales, row)
+        wd_rows = wd.rearrange("(p i) n -> p i n", i=PACK)
+        nc.sync.dma_start(wd_raw[0][:], wd_rows[:, :, 0 : N // 2])
         nc.sync.dma_start(sm_sb[:], sm.rearrange("(p i) -> p i", i=PACK))
-        nc.sync.dma_start(wd_raw[:], wd.rearrange("(p i) n -> p i n", i=PACK))
+        nc.sync.dma_start(wd_raw[1][:], wd_rows[:, :, N // 2 : N])
         nc.sync.dma_start(wgo_sb[:], wgo)
 
         windows = [sbuf([P, T], F32, "window%d" % n) for n in range(3)]
-        nc.gpsimd.memset(windows[0][:, 0 : 3 * T // 8], 0.0)
-        nc.gpsimd.dma_start(w_words[SRC][:], words(ws_words))
+        nc.gpsimd.memset(windows[0][:, 0 : 3 * T // 4], 0.0)
         nc.gpsimd.dma_start(w_words[DST][:], words(wt_words))
-        nc.gpsimd.memset(windows[0][:, 3 * T // 8 : T], 0.0)
+        nc.gpsimd.memset(windows[0][:, 3 * T // 4 : T], 0.0)
         nc.gpsimd.memset(windows[1][:], 0.0)
         nc.gpsimd.memset(windows[2][:], 0.0)
 
@@ -190,7 +191,7 @@ def tile_list_msg_silu_none_kernel(
             )
 
         def round_wd(n0, n1):
-            interleave(wd_grouped[:, n0 * P : n1 * P, :], wd_raw[:, :, n0 * P : n1 * P])
+            interleave(wd_grouped[n0 // 2][:], wd_raw[n0 // 2][:])
 
         def quantise_wd(n0, n1, at=None):
             codes = sbuf([P, (n1 - n0) * P], U32, "wd_codes%d" % n0)
@@ -198,7 +199,7 @@ def tile_list_msg_silu_none_kernel(
             nc.vector.quantize_mx(
                 out=codes[:].bitcast(FP8X4),
                 scales=scales[:],
-                in_=wd_grouped[:, n0 * P : n1 * P, :].rearrange("p n i -> p (n i)"),
+                in_=wd_grouped[n0 // 2][:].rearrange("p n i -> p (n i)"),
             )
             for n in range(n0, n1):
                 cols = slice((n - n0) * P, (n - n0 + 1) * P)
@@ -236,26 +237,25 @@ def tile_list_msg_silu_none_kernel(
 
         q0, q1, q2, q3, q4 = range(0, J + 1, QUARTER)
 
-        gather_scales(SRC, q0, q2)
-        gather_scales(DST, q0, q3)
+        gather_scales(DST, q0, q1, AT_FIRST_DST_SCALES)
+        gather_scales(SRC, q0, q4)
         gather_words(SRC, q0, q1, AT_FIRST_SRC_WORDS)
-        gather_words(DST, q0, q1)
-        gather_words(DST, q1, q4)
+        gather_words(DST, q0, q2)
         gather_words(SRC, q1, q4)
         project(0, 0)
-        project(0, 1, first=DST)
-        gather_scales(DST, q3, q4, AT_LAST_DST_SCALES)
+        project(0, 1)
+        gather_scales(DST, q1, q4, AT_LAST_DST_SCALES)
 
         activate(0, 0, parts=2)
-        activate(0, 1, at=AT_SECOND_SILU)
-        wd_grouped = sbuf([P, N, PACK], BF16, "wd_grouped", AT_WD_GROUPED)
+        activate(0, 1, parts=2, at=AT_SECOND_SILU)
+        wd_grouped = [sbuf([P, N // 2, PACK], BF16, "wd_grouped%d" % half, AT_WD_GROUPED[half]) for half in range(2)]
         round_wd(0, 2)
         round_wd(2, 4)
-        smooth_on_vector(0, AT_FIRST_HIDDEN)
+        smooth_on_vector(0, None)
         quantise_wd(0, 2, AT_WD_SCALES_FIRST)
         quantise_hidden(0)
+        gather_words(DST, q2, q4, AT_LAST_DST_WORDS)
         quantise_wd(2, 4)
-        gather_scales(SRC, q2, q4, AT_LAST_SRC_SCALES)
         windows.append(sbuf([P, T], F32, "window3", AT_LAST_WINDOW))
         nc.gpsimd.memset(windows[3][:], 0.0)
 

@@ -52,6 +52,7 @@ def tile_list_msg_silu_none_kernel(
         tab_plane = sbuf([P, T // 4], I32, "tab_plane")
         w_planes = [sbuf([P, R // 4], I32, "w_plane%d" % s) for s in (SRC, DST)]
         ident = sbuf([P, P], F32, "ident")
+        nc.vector.memset(tab_plane[96:P, :], 0)
         nc.gpsimd.memset(w_planes[SRC][:], 0)
         nc.gpsimd.memset(ident[:], 0.0)
         nc.gpsimd.memset(w_planes[DST][:], 0)
@@ -69,11 +70,12 @@ def tile_list_msg_silu_none_kernel(
         wgo_sb = sbuf([P, J], F32, "wgo_sb")
         sm_sb = sbuf([P, PACK], F32, "sm_sb")
 
-        for quadrant in range(4):
+        for quadrant in range(3):
             rows = tab_scales[0, 4 * quadrant : 4 * quadrant + 4].bitcast(I32)
-            queue = nc.sync if quadrant < 2 else nc.scalar
+            queue = nc.sync if quadrant == 0 else nc.scalar
             queue.dma_start(tab_plane[32 * quadrant : 32 * quadrant + 32, :], rows.unsqueeze(0).to_broadcast([8, 4, T // 4]))
         nc.sync.dma_start(lists[SRC][:], offs)
+        nc.sync.dma_start(tab_plane[96:100, :], tab_scales[0, 12:16].bitcast(I32))
         nc.sync.dma_start(tab[:], words(tab_words))
         load_scale_rows(nc.sync, w_planes[SRC], ws_scales, 0)
         nc.sync.dma_start(w_words[SRC][:], words(ws_words))

@@ -15,6 +15,7 @@ U8 = mybir.dt.uint8
 FP8X4 = mybir.dt.float8_e4m3fn_x4
 ACT = mybir.ActivationFunctionType
 MULT = mybir.AluOpType.mult
+ADD = mybir.AluOpType.add
 
 P = 128
 PACK = 4
@@ -23,13 +24,16 @@ BANK = 512
 SRC, DST = 0, 1
 
 AT_FIRST_SRC_WORDS = 0
-AT_LAST_DST_SCALES = AT_FIRST_SRC_WORDS
-AT_WD_GROUPED = (2048, 4096)
-AT_FIRST_DST_SCALES = AT_WD_GROUPED[1] - 128
-AT_LAST_DST_WORDS = AT_WD_GROUPED[0]
-AT_LAST_WINDOW = AT_WD_GROUPED[1]
-AT_SECOND_SILU = 16384
-AT_WD_SCALES_FIRST = AT_SECOND_SILU
+AT_LATE_SCALES = (0, 512)
+AT_SECOND_SILU = 1024
+AT_FIRST_PLANES = 6144
+AT_LATE_DST_WORDS = AT_FIRST_PLANES + 384 - 2048
+AT_WD_SCALES = (AT_SECOND_SILU, AT_FIRST_PLANES + 384)
+AT_THIRD_SILU = AT_FIRST_PLANES + 640
+AT_WD_SECOND_HALF = 9216
+AT_THIRD_WINDOW = AT_WD_SECOND_HALF
+AT_FIRST_Y = 17408
+AT_LAST_WINDOW = AT_FIRST_Y
 
 
 def tile_list_msg_silu_none_kernel(
@@ -89,19 +93,18 @@ def tile_list_msg_silu_none_kernel(
         nc.sync.dma_start(wd_raw[1][:], wd_rows[:, :, N // 2 : N])
         nc.sync.dma_start(wgo_sb[:], wgo)
 
-        windows = [sbuf([P, T], F32, "window%d" % n) for n in range(3)]
+        windows = [sbuf([P, T], F32, "window%d" % n) for n in range(2)]
         nc.gpsimd.memset(windows[0][:, 0 : 3 * T // 4], 0.0)
         nc.gpsimd.dma_start(w_words[DST][:], words(wt_words))
         nc.gpsimd.memset(windows[0][:, 3 * T // 4 : T], 0.0)
         nc.gpsimd.memset(windows[1][:], 0.0)
-        nc.gpsimd.memset(windows[2][:], 0.0)
 
         v_words = {}
         v_scales = {}
         sums = {}
         turned = {}
         h_planes = {}
-        h_grouped = {}
+        h_grouped = [sbuf([P, QUARTER, PACK], BF16, "h_grouped%d" % q) for q in range(4)]
         wd_mx = {}
         y_psum = {}
         h_codes = sbuf([P, J], U32, "h_codes")
@@ -114,7 +117,7 @@ def tile_list_msg_silu_none_kernel(
             tile = sbuf([P, j1 - j0], dtype, "%s%d_%d" % (name, s, j0), at)
             nc.vector.tensor_copy(tile[:], window[:].bitcast(dtype).indirect(offsets(s, j0, j1)))
             for j in range(j0, j1, P):
-                picked[s, j] = tile[:, j - j0 : j - j0 + P]
+                picked[s, j // P] = tile[:, j - j0 : j - j0 + P]
 
         def gather_scales(s, j0, j1, at=None):
             gather(v_scales, tab_plane, U8, "v_scales", s, j0, j1, at)
@@ -122,67 +125,52 @@ def tile_list_msg_silu_none_kernel(
         def gather_words(s, j0, j1, at=None):
             gather(v_words, tab, U32, "v_words", s, j0, j1, at)
 
-        def bank(q, tile, role):
-            swapped = q % 2 if tile == 0 else max(q - 1, 0) % 2
-            return "pair%d_%d" % (tile, (swapped + role) % 2)
-
-        def sum_bank(q, tile):
-            return bank(q, tile, 0)
-
-        def project(q, tile, first=SRC):
-            j = q * QUARTER + tile * P
-            sums[q, tile] = psum.tile([P, R], F32, name="sums", tag=sum_bank(q, tile))
-            for s in (first, 1 - first):
+        def project(t, bank):
+            sums[t] = psum.tile([P, R], F32, name="sums", tag=bank)
+            for s in (SRC, DST):
                 nc.tensor.matmul_mx(
-                    out=sums[q, tile][:],
-                    lhsT=v_words[s, j].bitcast(FP8X4),
-                    lhsT_scale=v_scales[s, j],
+                    out=sums[t][:],
+                    lhsT=v_words[s, t].bitcast(FP8X4),
+                    lhsT_scale=v_scales[s, t],
                     rhs=w_words[s][:].bitcast(FP8X4),
                     rhs_scale=w_planes[s][:].bitcast(U8),
-                    start=(s == first),
-                    stop=(s != first),
+                    start=(s == SRC),
+                    stop=(s == DST),
                 )
 
-        def activate(q, tile, parts=1, at=None):
-            act = sbuf([P, PACK, P], F32, "act%d_%d" % (q, tile), at)
-            turned[q, tile] = psum.tile([P, PACK, P], F32, name="turned", tag=bank(q, tile, 1))
-            by_plane = sums[q, tile][:].rearrange("j (p i) -> j i p", i=PACK)
+        def activate(t, bank, parts=1, at=None):
+            act = sbuf([P, PACK, P], F32, "act%d" % t, at)
+            turned[t] = psum.tile([P, PACK, P], F32, name="turned", tag=bank)
+            by_plane = sums[t][:].rearrange("j (p i) -> j i p", i=PACK)
             step = PACK // parts
             for i0 in range(0, PACK, step):
                 nc.scalar.activation(act[:, i0 : i0 + step, :], by_plane[:, i0 : i0 + step, :], ACT.Silu)
                 for i in range(i0, i0 + step):
-                    nc.tensor.transpose(turned[q, tile][:, i, :], act[:, i, :], ident[:])
+                    nc.tensor.transpose(turned[t][:, i, :], act[:, i, :], ident[:])
 
         def interleave(grouped, planes):
             nc.scalar.copy(
                 grouped.rearrange("p (c k) i -> p c i k", k=4), planes.rearrange("p i (c k) -> p c i k", k=4)
             )
 
-        def smooth_on_vector(q, at):
-            h_grouped[q] = sbuf([P, QUARTER, PACK], BF16, "h_grouped%d" % q, at)
-            for tile in range(2):
-                nc.vector.tensor_tensor(
-                    h_grouped[q][:, tile * P : (tile + 1) * P, :],
-                    turned[q, tile][:].rearrange("p i j -> p j i"),
-                    sm_sb[:].unsqueeze(1).to_broadcast([P, P, PACK]),
-                    MULT,
-                )
+        def grouped_tile(t):
+            return h_grouped[t // 2][:, (t % 2) * P : (t % 2 + 1) * P, :]
 
-        def scale_planes(q, tile):
+        def smooth_on_vector(t):
+            nc.vector.tensor_tensor(
+                grouped_tile(t),
+                turned[t][:].rearrange("p i j -> p j i"),
+                sm_sb[:].unsqueeze(1).to_broadcast([P, P, PACK]),
+                MULT,
+            )
+
+        def scale_planes(t, planes):
+            h_planes[t] = planes
             for i in range(PACK):
-                nc.scalar.activation(
-                    h_planes[q][:, i, tile * P : (tile + 1) * P],
-                    turned[q, tile][:, i, :],
-                    ACT.Copy,
-                    scale=sm_sb[:, i : i + 1],
-                )
+                nc.scalar.activation(planes[:, i, :], turned[t][:, i, :], ACT.Copy, scale=sm_sb[:, i : i + 1])
 
-        def smooth_on_scalar(q, tiles):
-            h_planes[q] = sbuf([P, PACK, QUARTER], BF16, "h_planes", tag="planes%d" % q)
-            for tile in tiles:
-                scale_planes(q, tile)
-            h_grouped[q] = sbuf([P, QUARTER, PACK], BF16, "h_grouped%d" % q)
-            interleave(h_grouped[q][:], h_planes[q][:])
+        def quarter_planes(q):
+            return sbuf([P, PACK, QUARTER], BF16, "h_planes", tag="planes%d" % q)
 
         def quantise_hidden(q):
             cols = slice(q * QUARTER, (q + 1) * QUARTER)
@@ -192,28 +180,25 @@ def tile_list_msg_silu_none_kernel(
                 in_=h_grouped[q][:].rearrange("p j i -> p (j i)"),
             )
 
-        def round_wd(n0, n1):
-            interleave(wd_grouped[n0 // 2][:], wd_raw[n0 // 2][:])
-
-        def quantise_wd(n0, n1, at=None):
-            codes = sbuf([P, (n1 - n0) * P], U32, "wd_codes%d" % n0)
-            scales = sbuf([P, (n1 - n0) * P], U8, "wd_scales%d" % n0, at)
+        def quantise_wd(half, at=None):
+            codes = sbuf([P, N // 2], U32, "wd_codes%d" % half)
+            scales = sbuf([P, N // 2], U8, "wd_scales%d" % half, at)
             nc.vector.quantize_mx(
                 out=codes[:].bitcast(FP8X4),
                 scales=scales[:],
-                in_=wd_grouped[n0 // 2][:].rearrange("p n i -> p (n i)"),
+                in_=wd_grouped[half][:].rearrange("p n i -> p (n i)"),
             )
-            for n in range(n0, n1):
-                cols = slice((n - n0) * P, (n - n0 + 1) * P)
-                wd_mx[n] = (codes[:, cols], scales[:, cols])
+            for n in range(2):
+                wd_mx[2 * half + n] = (codes[:, n * P : (n + 1) * P], scales[:, n * P : (n + 1) * P])
 
-        def message(n, j0, j1, y_bank):
-            y_psum[n, j0] = psum.tile([P, BANK], F32, name="y_psum", tag=y_bank)
-            product(y_psum[n, j0][:, 0 : j1 - j0], n, j0, j1)
+        def zeroed_window(n, at):
+            windows.append(sbuf([P, T], F32, "window%d" % n, at))
+            nc.gpsimd.memset(windows[n][:], 0.0)
 
-        def product(y_out, n, j0, j1):
+        def message(n, j0, j1, bank):
+            y_psum[n, j0] = psum.tile([P, BANK], F32, name="y_psum", tag=bank)
             nc.tensor.matmul_mx(
-                out=y_out,
+                out=y_psum[n, j0][:, 0 : j1 - j0],
                 lhsT=wd_mx[n][0].bitcast(FP8X4),
                 lhsT_scale=wd_mx[n][1],
                 rhs=h_codes[:, j0:j1].bitcast(FP8X4),
@@ -222,96 +207,93 @@ def tile_list_msg_silu_none_kernel(
                 stop=True,
             )
 
-        def scatter(n, j0, j1, y):
-            nc.vector.tensor_tensor(windows[n][:].indirect(offsets(DST, j0, j1)), y, wgo_sb[:, j0:j1], MULT)
-
         def place(n, j0, j1, tag="", at=None):
             y = sbuf([P, j1 - j0], F32, "y%d_%d" % (n, j0), at, tag)
             nc.scalar.copy(y[:], y_psum[n, j0][:, 0 : j1 - j0])
-            scatter(n, j0, j1, y[:])
+            nc.vector.tensor_tensor(windows[n][:].indirect(offsets(DST, j0, j1)), y[:], wgo_sb[:, j0:j1], MULT)
 
-        def piece(n, j0, j1, y_bank, tag=""):
-            message(n, j0, j1, y_bank)
+        def piece(n, j0, j1, bank, tag=""):
+            message(n, j0, j1, bank)
             place(n, j0, j1, tag)
 
         def store(n):
             nc.sync.dma_start(out[n * P : (n + 1) * P, :], windows[n][:])
 
         q0, q1, q2, q3, q4 = range(0, J + 1, QUARTER)
+        lo, hi = slice(0, P), slice(P, QUARTER)
 
-        gather_scales(DST, q0, q1, AT_FIRST_DST_SCALES)
-        gather_scales(SRC, q0, q4)
+        gather_scales(DST, q0, q2)
+        gather_scales(SRC, q0, q2)
         gather_words(SRC, q0, q1, AT_FIRST_SRC_WORDS)
         gather_words(DST, q0, q2)
         gather_words(SRC, q1, q4)
-        project(0, 0)
-        project(0, 1)
-        gather_scales(DST, q1, q4, AT_LAST_DST_SCALES)
+        project(0, "a0")
+        project(1, "a1")
+        gather_scales(SRC, q2, q4, AT_LATE_SCALES[SRC])
+        gather_scales(DST, q2, q4, AT_LATE_SCALES[DST])
 
-        activate(0, 0, parts=2)
-        activate(0, 1, parts=2, at=AT_SECOND_SILU)
-        wd_grouped = [sbuf([P, N // 2, PACK], BF16, "wd_grouped%d" % half, AT_WD_GROUPED[half]) for half in range(2)]
-        round_wd(0, 2)
-        round_wd(2, 4)
-        smooth_on_vector(0, None)
-        quantise_wd(0, 2, AT_WD_SCALES_FIRST)
+        wd_grouped = [sbuf([P, N // 2, PACK], BF16, "wd_grouped0"), sbuf([P, N // 2, PACK], BF16, "wd_grouped1", AT_WD_SECOND_HALF)]
+        for half in range(2):
+            nc.gpsimd.tensor_scalar(wd_grouped[half][:], wd_raw[half][:].rearrange("p i n -> p n i"), 1.0, 0.0, MULT, ADD)
+        activate(0, "b0", parts=2)
+        activate(1, "b1", parts=2, at=AT_SECOND_SILU)
+        first_planes = sbuf([P, PACK, P], BF16, "first_planes", AT_FIRST_PLANES)
+        scale_planes(0, first_planes[:])
+        interleave(grouped_tile(0), first_planes[:])
+        smooth_on_vector(1)
+        quantise_wd(0, AT_WD_SCALES[0])
         quantise_hidden(0)
-        gather_words(DST, q2, q4, AT_LAST_DST_WORDS)
-        quantise_wd(2, 4)
-        windows.append(sbuf([P, T], F32, "window3", AT_LAST_WINDOW))
-        nc.gpsimd.memset(windows[3][:], 0.0)
+        gather_words(DST, q2, q4, AT_LATE_DST_WORDS)
+        quantise_wd(1, AT_WD_SCALES[1])
+        zeroed_window(2, AT_THIRD_WINDOW)
 
-        message(0, q0, q1, "y0")
-        project(1, 1)
-        project(1, 0)
-        activate(1, 1)
-        activate(1, 0)
-        place(0, q0, q1)
-        piece(1, q0, q1, sum_bank(1, 0))
-        piece(2, q0, q1, "y0")
-        smooth_on_scalar(1, (1, 0))
+        message(0, q0, q1, "c0")
+        project(3, "a1")
+        project(2, "b0")
+        activate(3, "b1", at=AT_THIRD_SILU)
+        activate(2, "a0")
+        place(0, q0, q1, at=AT_FIRST_Y)
+        zeroed_window(3, AT_LAST_WINDOW)
+        piece(1, q0, q1, "b0")
+        piece(2, q0, q1, "c0")
+        planes = quarter_planes(1)
+        scale_planes(3, planes[:, :, hi])
+        scale_planes(2, planes[:, :, lo])
+        interleave(h_grouped[1][:], planes[:])
         quantise_hidden(1)
-        piece(3, q0, q1, sum_bank(1, 0), "planes1")
+        piece(3, q0, q1, "b0", "planes1")
 
-        def planes_tile(q):
-            h_planes[q] = sbuf([P, PACK, QUARTER], BF16, "h_planes", tag="planes%d" % q)
-
-        def group(q):
-            h_grouped[q] = sbuf([P, QUARTER, PACK], BF16, "h_grouped%d" % q)
-            interleave(h_grouped[q][:], h_planes[q][:])
-
-        project(2, 1)
-        project(2, 0)
-        activate(2, 1)
-        message(0, q1, q2, sum_bank(2, 1))
-        activate(2, 0)
+        project(5, "b1")
+        project(4, "a0")
+        activate(5, "a1")
+        message(0, q1, q2, "b1")
+        activate(4, "b0")
         place(0, q1, q2)
-        planes_tile(2)
-        scale_planes(2, 1)
-        piece(1, q1, q2, sum_bank(2, 0))
-        scale_planes(2, 0)
-        piece(2, q1, q2, sum_bank(2, 1))
-        group(2)
+        planes = quarter_planes(2)
+        scale_planes(5, planes[:, :, hi])
+        piece(1, q1, q2, "a0")
+        scale_planes(4, planes[:, :, lo])
+        piece(2, q1, q2, "b1")
+        interleave(h_grouped[2][:], planes[:])
         quantise_hidden(2)
-        piece(3, q1, q2, sum_bank(2, 0), "planes2")
+        piece(3, q1, q2, "a0", "planes2")
 
-        project(3, 1)
-        project(3, 0)
-        activate(3, 1)
-        activate(3, 0)
-        planes_tile(3)
-        scale_planes(3, 1)
-        scale_planes(3, 0)
-        h_grouped[3] = sbuf([P, QUARTER, PACK], BF16, "h_grouped3")
-        interleave(h_grouped[3][:, P : 2 * P, :], h_planes[3][:, :, P : 2 * P])
-        piece(0, q2, q3, sum_bank(3, 0))
-        interleave(h_grouped[3][:, 0:P, :], h_planes[3][:, :, 0:P])
+        project(7, "a1")
+        project(6, "b0")
+        activate(7, "b1")
+        activate(6, "a0")
+        planes = quarter_planes(3)
+        scale_planes(7, planes[:, :, hi])
+        scale_planes(6, planes[:, :, lo])
+        interleave(grouped_tile(7), planes[:, :, hi])
+        piece(0, q2, q3, "b0")
+        interleave(grouped_tile(6), planes[:, :, lo])
         quantise_hidden(3)
-        piece(1, q2, q3, sum_bank(3, 0), "planes3")
+        piece(1, q2, q3, "b0", "planes3")
 
         for n in range(2):
-            piece(n, q3, q4, "y%d" % n)
+            piece(n, q3, q4, "c%d" % n)
             store(n)
         for n in range(2, 4):
-            piece(n, q2, q4, "y%d" % n)
+            piece(n, q2, q4, "c%d" % n)
             store(n)

@@ -18,6 +18,7 @@ MULT = mybir.AluOpType.mult
 ADD = mybir.AluOpType.add
 
 P = 128
+DMA_ALIGN = 256
 PACK = 4
 QUARTER = J // 4
 BANK = 512
@@ -34,6 +35,9 @@ AT_WD_SECOND_HALF = 9216
 AT_THIRD_WINDOW = AT_WD_SECOND_HALF
 AT_FIRST_Y = 17408
 AT_LAST_WINDOW = AT_FIRST_Y
+AT_THIRD_PLANES = 28672
+AT_HELD_Y = AT_THIRD_PLANES + 64
+AT_LAST_SILUS = (AT_HELD_Y - 2048, AT_HELD_Y + 1024)
 
 
 def tile_list_msg_silu_none_kernel(
@@ -45,16 +49,16 @@ def tile_list_msg_silu_none_kernel(
         shared = ctx.enter_context(tc.tile_pool(name="shared", bufs=1))
         psum = ctx.enter_context(tc.psum_pool(name="psum", bufs=1))
 
-        def sbuf(shape, dtype, name, at=None, tag=""):
+        def sbuf(shape, dtype, name, at=None, tag="", align=64):
             if at is None:
-                return keep.tile(shape, dtype, name=name, tag=tag, align_bytes=64)
-            return shared.tile(shape, dtype, name=name, offset=at, align_bytes=64)
+                return keep.tile(shape, dtype, name=name, tag=tag, align_bytes=align)
+            return shared.tile(shape, dtype, name=name, offset=at, align_bytes=align)
 
         lists = [keep.tile([P, J // 16], U16, name="list%d" % s) for s in (SRC, DST)]
         nc.sync.dma_start(lists[DST][:], offs2)
 
-        tab_plane = sbuf([P, T // 4], I32, "tab_plane")
-        w_planes = [sbuf([P, R // 4], I32, "w_plane%d" % s) for s in (SRC, DST)]
+        tab_plane = sbuf([P, T // 4], I32, "tab_plane", align=DMA_ALIGN)
+        w_planes = [sbuf([P, R // 4], I32, "w_plane%d" % s, align=DMA_ALIGN) for s in (SRC, DST)]
         ident = sbuf([P, P], F32, "ident")
         nc.vector.memset(tab_plane[96:P, :], 0)
         nc.gpsimd.memset(w_planes[SRC][:], 0)
@@ -68,10 +72,10 @@ def tile_list_msg_silu_none_kernel(
         def words(packed):
             return packed[0].rearrange("p c i -> p (c i)").bitcast(I32)
 
-        tab = sbuf([P, T], I32, "tab")
-        w_words = [sbuf([P, R], I32, "w_words%d" % s) for s in (SRC, DST)]
-        wd_raw = [sbuf([P, PACK, N // 2], F32, "wd_raw0"), sbuf([P, PACK, N // 2], F32, "wd_raw1")]
-        wgo_sb = sbuf([P, J], F32, "wgo_sb")
+        tab = sbuf([P, T], I32, "tab", align=DMA_ALIGN)
+        w_words = [sbuf([P, R], I32, "w_words%d" % s, align=DMA_ALIGN) for s in (SRC, DST)]
+        wd_raw = [sbuf([P, PACK, N // 2], F32, "wd_raw%d" % half, align=DMA_ALIGN) for half in range(2)]
+        wgo_sb = sbuf([P, J], F32, "wgo_sb", align=DMA_ALIGN)
         sm_sb = sbuf([P, PACK], F32, "sm_sb")
 
         for quadrant in range(3):
@@ -93,7 +97,7 @@ def tile_list_msg_silu_none_kernel(
         nc.sync.dma_start(wd_raw[1][:], wd_rows[:, :, N // 2 : N])
         nc.sync.dma_start(wgo_sb[:], wgo)
 
-        windows = [sbuf([P, T], F32, "window%d" % n) for n in range(2)]
+        windows = [sbuf([P, T], F32, "window%d" % n, align=DMA_ALIGN) for n in range(2)]
         nc.gpsimd.memset(windows[0][:, 0 : 3 * T // 4], 0.0)
         nc.gpsimd.dma_start(w_words[DST][:], words(wt_words))
         nc.gpsimd.memset(windows[0][:, 3 * T // 4 : T], 0.0)
@@ -192,7 +196,7 @@ def tile_list_msg_silu_none_kernel(
                 wd_mx[2 * half + n] = (codes[:, n * P : (n + 1) * P], scales[:, n * P : (n + 1) * P])
 
         def zeroed_window(n, at):
-            windows.append(sbuf([P, T], F32, "window%d" % n, at))
+            windows.append(sbuf([P, T], F32, "window%d" % n, at, align=DMA_ALIGN))
             nc.gpsimd.memset(windows[n][:], 0.0)
 
         def message(n, j0, j1, bank):
@@ -207,10 +211,16 @@ def tile_list_msg_silu_none_kernel(
                 stop=True,
             )
 
+        def copy_out(y, n, j0, j1):
+            nc.scalar.copy(y, y_psum[n, j0][:, 0 : j1 - j0])
+
+        def scatter(n, j0, j1, y):
+            nc.vector.tensor_tensor(windows[n][:].indirect(offsets(DST, j0, j1)), y, wgo_sb[:, j0:j1], MULT)
+
         def place(n, j0, j1, tag="", at=None):
             y = sbuf([P, j1 - j0], F32, "y%d_%d" % (n, j0), at, tag)
-            nc.scalar.copy(y[:], y_psum[n, j0][:, 0 : j1 - j0])
-            nc.vector.tensor_tensor(windows[n][:].indirect(offsets(DST, j0, j1)), y[:], wgo_sb[:, j0:j1], MULT)
+            copy_out(y[:], n, j0, j1)
+            scatter(n, j0, j1, y[:])
 
         def piece(n, j0, j1, bank, tag=""):
             message(n, j0, j1, bank)
@@ -254,11 +264,11 @@ def tile_list_msg_silu_none_kernel(
         activate(2, "a0")
         place(0, q0, q1, at=AT_FIRST_Y)
         zeroed_window(3, AT_LAST_WINDOW)
-        piece(1, q0, q1, "b0")
-        piece(2, q0, q1, "c0")
         planes = quarter_planes(1)
         scale_planes(3, planes[:, :, hi])
+        piece(1, q0, q1, "b0")
         scale_planes(2, planes[:, :, lo])
+        piece(2, q0, q1, "c0")
         interleave(h_grouped[1][:], planes[:])
         quantise_hidden(1)
         piece(3, q0, q1, "b0", "planes1")
@@ -266,34 +276,38 @@ def tile_list_msg_silu_none_kernel(
         project(5, "b1")
         project(4, "a0")
         activate(5, "a1")
-        message(0, q1, q2, "b1")
         activate(4, "b0")
-        place(0, q1, q2)
-        planes = quarter_planes(2)
+        message(0, q1, q2, "a0")
+        planes = sbuf([P, PACK, QUARTER], BF16, "third_planes", AT_THIRD_PLANES)
         scale_planes(5, planes[:, :, hi])
-        piece(1, q1, q2, "a0")
+        place(0, q1, q2)
         scale_planes(4, planes[:, :, lo])
-        piece(2, q1, q2, "b1")
+        piece(1, q1, q2, "a0")
         interleave(h_grouped[2][:], planes[:])
         quantise_hidden(2)
-        piece(3, q1, q2, "a0", "planes2")
+        message(2, q1, q2, "a0")
+        place(2, q1, q2, at=AT_HELD_Y)
 
+        y_wide = sbuf([P, 2 * QUARTER], F32, "y_wide")
+        message(3, q1, q2, "a0")
+        message(3, q2, q3, "c0")
         project(7, "a1")
         project(6, "b0")
-        activate(7, "b1")
-        activate(6, "a0")
+        activate(7, "b1", at=AT_LAST_SILUS[1])
+        activate(6, "c1", at=AT_LAST_SILUS[0])
+        copy_out(y_wide[:, 0:QUARTER], 3, q1, q2)
+        copy_out(y_wide[:, QUARTER : 2 * QUARTER], 3, q2, q3)
+        scatter(3, q1, q3, y_wide[:])
         planes = quarter_planes(3)
         scale_planes(7, planes[:, :, hi])
         scale_planes(6, planes[:, :, lo])
-        interleave(grouped_tile(7), planes[:, :, hi])
-        piece(0, q2, q3, "b0")
-        interleave(grouped_tile(6), planes[:, :, lo])
+        interleave(h_grouped[3][:], planes[:])
         quantise_hidden(3)
-        piece(1, q2, q3, "b0", "planes3")
+        piece(0, q2, q3, "b0", "planes3")
 
-        for n in range(2):
-            piece(n, q3, q4, "c%d" % n)
+        for n in (3, 0):
+            piece(n, q3, q4, "c%d" % (n % 2))
             store(n)
-        for n in range(2, 4):
-            piece(n, q2, q4, "c%d" % n)
+        for n in (1, 2):
+            piece(n, q2, q4, "c%d" % (n % 2))
             store(n)

from contextlib import ExitStack

import concourse.mybir as mybir
from concourse.masks import make_identity

K, R, N, T, J = 512, 512, 512, 2048, 1024
FLOPS = 2 * (2 * K * R * J + R * N * J)

F32 = mybir.dt.float32
BF16 = mybir.dt.bfloat16
I32 = mybir.dt.int32
U32 = mybir.dt.uint32
U16 = mybir.dt.uint16
U8 = mybir.dt.uint8
FP8X4 = mybir.dt.float8_e4m3fn_x4
ACT = mybir.ActivationFunctionType
MULT = mybir.AluOpType.mult
ADD = mybir.AluOpType.add

P = 128
DMA_ALIGN = 256
PACK = 4
QUARTER = J // 4
BANK = 512
SRC, DST = 0, 1

AT_FIRST_SRC_WORDS = 0
AT_LATE_SCALES = (0, 512)
AT_SECOND_SILU = 1024
AT_FIRST_PLANES = 6144
AT_LATE_DST_WORDS = AT_FIRST_PLANES + 384 - 2048
AT_WD_SCALES = (AT_SECOND_SILU, AT_FIRST_PLANES + 384)
AT_THIRD_SILU = AT_FIRST_PLANES + 640
AT_WD_SECOND_HALF = 9216
AT_THIRD_WINDOW = AT_WD_SECOND_HALF
AT_FIRST_Y = 17408
AT_LAST_WINDOW = AT_FIRST_Y
AT_THIRD_PLANES = 28672
AT_HELD_Y = AT_THIRD_PLANES + 64
AT_LAST_SILUS = (AT_HELD_Y - 2048, AT_HELD_Y + 1024)


def tile_list_msg_silu_none_kernel(
    tc, tab_words, tab_scales, ws_words, ws_scales, wt_words, wt_scales, sm, wd, wgo, offs, offs2, out
):
    nc = tc.nc
    with ExitStack() as ctx:
        keep = ctx.enter_context(tc.tile_pool(name="keep", bufs=1))
        shared = ctx.enter_context(tc.tile_pool(name="shared", bufs=1))
        psum = ctx.enter_context(tc.psum_pool(name="psum", bufs=1))

        def sbuf(shape, dtype, name, at=None, tag="", align=64):
            if at is None:
                return keep.tile(shape, dtype, name=name, tag=tag, align_bytes=align)
            return shared.tile(shape, dtype, name=name, offset=at, align_bytes=align)

        lists = [keep.tile([P, J // 16], U16, name="list%d" % s) for s in (SRC, DST)]
        nc.sync.dma_start(lists[DST][:], offs2)

        tab_plane = sbuf([P, T // 4], I32, "tab_plane", align=DMA_ALIGN)
        w_planes = [sbuf([P, R // 4], I32, "w_plane%d" % s, align=DMA_ALIGN) for s in (SRC, DST)]
        ident = sbuf([P, P], F32, "ident")
        nc.vector.memset(tab_plane[96:P, :], 0)
        nc.gpsimd.memset(w_planes[SRC][:], 0)
        nc.gpsimd.memset(ident[:], 0.0)
        nc.gpsimd.memset(w_planes[DST][:], 0)
        make_identity(nc, ident[:], nomemset=True)

        def load_scale_rows(queue, plane, scales, row):
            queue.dma_start(plane[row:P:32, :], scales[0].rearrange("(q r) c -> r q c", r=4)[row].bitcast(I32))

        def words(packed):
            return packed[0].rearrange("p c i -> p (c i)").bitcast(I32)

        tab = sbuf([P, T], I32, "tab", align=DMA_ALIGN)
        w_words = [sbuf([P, R], I32, "w_words%d" % s, align=DMA_ALIGN) for s in (SRC, DST)]
        wd_raw = [sbuf([P, PACK, N // 2], F32, "wd_raw%d" % half, align=DMA_ALIGN) for half in range(2)]
        wgo_sb = sbuf([P, J], F32, "wgo_sb", align=DMA_ALIGN)
        sm_sb = sbuf([P, PACK], F32, "sm_sb")

        for quadrant in range(3):
            rows = tab_scales[0, 4 * quadrant : 4 * quadrant + 4].bitcast(I32)
            queue = nc.sync if quadrant == 0 else nc.scalar
            queue.dma_start(tab_plane[32 * quadrant : 32 * quadrant + 32, :], rows.unsqueeze(0).to_broadcast([8, 4, T // 4]))
        nc.sync.dma_start(lists[SRC][:], offs)
        nc.sync.dma_start(tab_plane[96:100, :], tab_scales[0, 12:16].bitcast(I32))
        nc.sync.dma_start(tab[:], words(tab_words))
        load_scale_rows(nc.sync, w_planes[SRC], ws_scales, 0)
        nc.sync.dma_start(w_words[SRC][:], words(ws_words))
        for row in range(1, 4):
            load_scale_rows(nc.sync, w_planes[SRC], ws_scales, row)
        for row in range(4):
            load_scale_rows(nc.sync, w_planes[DST], wt_scales, row)
        wd_rows = wd.rearrange("(p i) n -> p i n", i=PACK)
        nc.sync.dma_start(wd_raw[0][:], wd_rows[:, :, 0 : N // 2])
        nc.sync.dma_start(sm_sb[:], sm.rearrange("(p i) -> p i", i=PACK))
        nc.sync.dma_start(wd_raw[1][:], wd_rows[:, :, N // 2 : N])
        nc.sync.dma_start(wgo_sb[:], wgo)

        windows = [sbuf([P, T], F32, "window%d" % n, align=DMA_ALIGN) for n in range(2)]
        nc.gpsimd.memset(windows[0][:, 0 : 3 * T // 4], 0.0)
        nc.gpsimd.dma_start(w_words[DST][:], words(wt_words))
        nc.gpsimd.memset(windows[0][:, 3 * T // 4 : T], 0.0)
        nc.gpsimd.memset(windows[1][:], 0.0)

        v_words = {}
        v_scales = {}
        sums = {}
        turned = {}
        h_planes = {}
        h_grouped = [sbuf([P, QUARTER, PACK], BF16, "h_grouped%d" % q) for q in range(4)]
        wd_mx = {}
        y_psum = {}
        h_codes = sbuf([P, J], U32, "h_codes")
        h_scales = sbuf([P, J], U8, "h_scales")

        def offsets(s, j0, j1):
            return lists[s][:, j0 // 16 : j1 // 16]

        def gather(picked, window, dtype, name, s, j0, j1, at):
            tile = sbuf([P, j1 - j0], dtype, "%s%d_%d" % (name, s, j0), at)
            nc.vector.tensor_copy(tile[:], window[:].bitcast(dtype).indirect(offsets(s, j0, j1)))
            for j in range(j0, j1, P):
                picked[s, j // P] = tile[:, j - j0 : j - j0 + P]

        def gather_scales(s, j0, j1, at=None):
            gather(v_scales, tab_plane, U8, "v_scales", s, j0, j1, at)

        def gather_words(s, j0, j1, at=None):
            gather(v_words, tab, U32, "v_words", s, j0, j1, at)

        def project(t, bank):
            sums[t] = psum.tile([P, R], F32, name="sums", tag=bank)
            for s in (SRC, DST):
                nc.tensor.matmul_mx(
                    out=sums[t][:],
                    lhsT=v_words[s, t].bitcast(FP8X4),
                    lhsT_scale=v_scales[s, t],
                    rhs=w_words[s][:].bitcast(FP8X4),
                    rhs_scale=w_planes[s][:].bitcast(U8),
                    start=(s == SRC),
                    stop=(s == DST),
                )

        def activate(t, bank, parts=1, at=None):
            act = sbuf([P, PACK, P], F32, "act%d" % t, at)
            turned[t] = psum.tile([P, PACK, P], F32, name="turned", tag=bank)
            by_plane = sums[t][:].rearrange("j (p i) -> j i p", i=PACK)
            step = PACK // parts
            for i0 in range(0, PACK, step):
                nc.scalar.activation(act[:, i0 : i0 + step, :], by_plane[:, i0 : i0 + step, :], ACT.Silu)
                for i in range(i0, i0 + step):
                    nc.tensor.transpose(turned[t][:, i, :], act[:, i, :], ident[:])

        def interleave(grouped, planes):
            nc.scalar.copy(
                grouped.rearrange("p (c k) i -> p c i k", k=4), planes.rearrange("p i (c k) -> p c i k", k=4)
            )

        def grouped_tile(t):
            return h_grouped[t // 2][:, (t % 2) * P : (t % 2 + 1) * P, :]

        def smooth_on_vector(t):
            nc.vector.tensor_tensor(
                grouped_tile(t),
                turned[t][:].rearrange("p i j -> p j i"),
                sm_sb[:].unsqueeze(1).to_broadcast([P, P, PACK]),
                MULT,
            )

        def scale_planes(t, planes):
            h_planes[t] = planes
            for i in range(PACK):
                nc.scalar.activation(planes[:, i, :], turned[t][:, i, :], ACT.Copy, scale=sm_sb[:, i : i + 1])

        def quarter_planes(q):
            return sbuf([P, PACK, QUARTER], BF16, "h_planes", tag="planes%d" % q)

        def quantise_hidden(q):
            cols = slice(q * QUARTER, (q + 1) * QUARTER)
            nc.vector.quantize_mx(
                out=h_codes[:, cols].bitcast(FP8X4),
                scales=h_scales[:, cols],
                in_=h_grouped[q][:].rearrange("p j i -> p (j i)"),
            )

        def quantise_wd(half, at=None):
            codes = sbuf([P, N // 2], U32, "wd_codes%d" % half)
            scales = sbuf([P, N // 2], U8, "wd_scales%d" % half, at)
            nc.vector.quantize_mx(
                out=codes[:].bitcast(FP8X4),
                scales=scales[:],
                in_=wd_grouped[half][:].rearrange("p n i -> p (n i)"),
            )
            for n in range(2):
                wd_mx[2 * half + n] = (codes[:, n * P : (n + 1) * P], scales[:, n * P : (n + 1) * P])

        def zeroed_window(n, at):
            windows.append(sbuf([P, T], F32, "window%d" % n, at, align=DMA_ALIGN))
            nc.gpsimd.memset(windows[n][:], 0.0)

        def message(n, j0, j1, bank):
            y_psum[n, j0] = psum.tile([P, BANK], F32, name="y_psum", tag=bank)
            nc.tensor.matmul_mx(
                out=y_psum[n, j0][:, 0 : j1 - j0],
                lhsT=wd_mx[n][0].bitcast(FP8X4),
                lhsT_scale=wd_mx[n][1],
                rhs=h_codes[:, j0:j1].bitcast(FP8X4),
                rhs_scale=h_scales[:, j0:j1],
                start=True,
                stop=True,
            )

        def copy_out(y, n, j0, j1):
            nc.scalar.copy(y, y_psum[n, j0][:, 0 : j1 - j0])

        def scatter(n, j0, j1, y):
            nc.vector.tensor_tensor(windows[n][:].indirect(offsets(DST, j0, j1)), y, wgo_sb[:, j0:j1], MULT)

        def place(n, j0, j1, tag="", at=None):
            y = sbuf([P, j1 - j0], F32, "y%d_%d" % (n, j0), at, tag)
            copy_out(y[:], n, j0, j1)
            scatter(n, j0, j1, y[:])

        def piece(n, j0, j1, bank, tag=""):
            message(n, j0, j1, bank)
            place(n, j0, j1, tag)

        def store(n):
            nc.sync.dma_start(out[n * P : (n + 1) * P, :], windows[n][:])

        q0, q1, q2, q3, q4 = range(0, J + 1, QUARTER)
        lo, hi = slice(0, P), slice(P, QUARTER)

        gather_scales(DST, q0, q2)
        gather_scales(SRC, q0, q2)
        gather_words(SRC, q0, q1, AT_FIRST_SRC_WORDS)
        gather_words(DST, q0, q2)
        gather_words(SRC, q1, q4)
        project(0, "a0")
        project(1, "a1")
        gather_scales(SRC, q2, q4, AT_LATE_SCALES[SRC])
        gather_scales(DST, q2, q4, AT_LATE_SCALES[DST])

        wd_grouped = [sbuf([P, N // 2, PACK], BF16, "wd_grouped0"), sbuf([P, N // 2, PACK], BF16, "wd_grouped1", AT_WD_SECOND_HALF)]
        for half in range(2):
            nc.gpsimd.tensor_scalar(wd_grouped[half][:], wd_raw[half][:].rearrange("p i n -> p n i"), 1.0, 0.0, MULT, ADD)
        activate(0, "b0", parts=2)
        activate(1, "b1", parts=2, at=AT_SECOND_SILU)
        first_planes = sbuf([P, PACK, P], BF16, "first_planes", AT_FIRST_PLANES)
        scale_planes(0, first_planes[:])
        interleave(grouped_tile(0), first_planes[:])
        smooth_on_vector(1)
        quantise_wd(0, AT_WD_SCALES[0])
        quantise_hidden(0)
        gather_words(DST, q2, q4, AT_LATE_DST_WORDS)
        quantise_wd(1, AT_WD_SCALES[1])
        zeroed_window(2, AT_THIRD_WINDOW)

        message(0, q0, q1, "c0")
        project(3, "a1")
        project(2, "b0")
        activate(3, "b1", at=AT_THIRD_SILU)
        activate(2, "a0")
        place(0, q0, q1, at=AT_FIRST_Y)
        zeroed_window(3, AT_LAST_WINDOW)
        planes = quarter_planes(1)
        scale_planes(3, planes[:, :, hi])
        piece(1, q0, q1, "b0")
        scale_planes(2, planes[:, :, lo])
        piece(2, q0, q1, "c0")
        interleave(h_grouped[1][:], planes[:])
        quantise_hidden(1)
        piece(3, q0, q1, "b0", "planes1")

        project(5, "b1")
        project(4, "a0")
        activate(5, "a1")
        activate(4, "b0")
        message(0, q1, q2, "a0")
        planes = sbuf([P, PACK, QUARTER], BF16, "third_planes", AT_THIRD_PLANES)
        scale_planes(5, planes[:, :, hi])
        place(0, q1, q2)
        scale_planes(4, planes[:, :, lo])
        piece(1, q1, q2, "a0")
        interleave(h_grouped[2][:], planes[:])
        quantise_hidden(2)
        message(2, q1, q2, "a0")
        place(2, q1, q2, at=AT_HELD_Y)

        y_wide = sbuf([P, 2 * QUARTER], F32, "y_wide")
        message(3, q1, q2, "a0")
        message(3, q2, q3, "c0")
        project(7, "a1")
        project(6, "b0")
        activate(7, "b1", at=AT_LAST_SILUS[1])
        activate(6, "c1", at=AT_LAST_SILUS[0])
        copy_out(y_wide[:, 0:QUARTER], 3, q1, q2)
        copy_out(y_wide[:, QUARTER : 2 * QUARTER], 3, q2, q3)
        scatter(3, q1, q3, y_wide[:])
        planes = quarter_planes(3)
        scale_planes(7, planes[:, :, hi])
        scale_planes(6, planes[:, :, lo])
        interleave(h_grouped[3][:], planes[:])
        quantise_hidden(3)
        piece(0, q2, q3, "b0", "planes3")

        for n in (3, 0):
            piece(n, q3, q4, "c%d" % (n % 2))
            store(n)
        for n in (1, 2):
            piece(n, q2, q4, "c%d" % (n % 2))
            store(n)
